import numpy as np, ml_dtypes
CORES = [40,41,42,43,44,45,46,47]
N = 8
BF = ml_dtypes.bfloat16
W, K, E, TH, ST, RO = 8192, 512, 16, 8, 3, 3
def subset(rng, cnt):
    a = 2 * rng.integers(0, 8, cnt.shape) + 1; o = rng.integers(0, 16, cnt.shape)
    return (((a * np.arange(16)[:, None] + o) & 15) < cnt).astype(np.int16)
def parts(rng):
    x = rng.integers(0, 256, (N, 8, 1, W), dtype=np.int16) + rng.integers(-12, 13, (N, 8, 16, W), dtype=np.int16)
    x = np.where(rng.random((N, 8, 1, W)) < 0.125, rng.integers(0, 256, (N, 8, 16, W), dtype=np.int16), np.clip(x, 0, 255))
    stk = rng.integers(0, W, (N, 8, 16, K)); bas = rng.integers(0, W, (N, 8, 16, K)); con = rng.integers(0, W, (N, 8, 16, K)); ln = rng.integers(1, 16, (N, 8, K))
    lv = (255.0 * (1.0 - rng.random((N, 8, 1, K)) ** 2)).astype(np.int64)
    z = np.clip(lv + rng.integers(-12, 13, (N, 8, 16, K)), 0, 255); w = rng.integers(1, 258, (N, 8, 16, 1))
    return x, stk, bas, con, ln, z, w
def pack(x, stk, bas, con, ln, z, w):
    def t(a, n): return np.ascontiguousarray(np.reshape(a, (N, 128, n)))
    return {"xt": t(x, W).astype(np.float32).astype(BF), "stk": t(stk, K).astype(np.int32), "bas": t(bas, K).astype(np.int32), "con": t(con, K).astype(np.int32),
            "ln": np.ascontiguousarray(ln).astype(np.int32), "z": t(z, K).astype(np.float32).astype(BF), "w": t(w, 1).astype(np.int32)}
def setup_inputs(rng):
    return pack(*parts(rng))
def setup_inputs_spread(rng):
    x, stk, bas, con, ln, z, w = parts(rng)
    x = (np.exp2(8.0 * rng.random((N, 8, 1, W), dtype=np.float32)) * rng.random((N, 8, 16, W), dtype=np.float32)).astype(np.int16)
    x = np.minimum(x, 255) * (rng.random((N, 8, 1, W)) > 0.0625)
    z = np.minimum((np.exp2(8.0 * rng.random((N, 8, 1, K))) * rng.random((N, 8, 16, K))).astype(np.int64), 255)
    def skew(lo, n, shape):
        e = rng.choice(np.array([0.25, 1.0, 4.0]), (N, 8) + (1,) * (len(shape) - 2))
        return np.minimum(lo + (n * rng.random(shape) ** e).astype(np.int64), lo + n - 1)
    stk = skew(0, W, (N, 8, 16, K)); bas = skew(0, W, (N, 8, 16, K)); con = skew(0, W, (N, 8, 16, K)); ln = skew(1, 15, (N, 8, K))
    w = np.minimum(np.exp2(8.01 * rng.random((N, 8, 16, 1))).astype(np.int64), 257)
    return pack(x, stk, bas, con, ln, z, w)
def endnames(rng):
    a = (W - 1) * rng.integers(0, 2, (N, 8, 16, K))
    s = (W - 1) * ((np.arange(16)[:, None] >= rng.integers(0, 17, (N, 8, 1, K))).astype(np.int64) ^ rng.integers(0, 2, (N, 8, 1, K)))
    ty = rng.random((N, 8, 1, K))
    return np.where(ty < 0.4, a, np.where(ty < 0.75, s, rng.integers(0, W, (N, 8, 16, K))))
def setup_inputs_ends(rng):
    cnt = rng.choice(np.array([0, 1, TH - 2, TH - 1, TH, 12, 16]), (N, 8, 1, W)); cnt[1] = np.minimum(cnt[1], TH - 2)
    x = 255 * subset(rng, cnt)
    zc = rng.choice(np.array([0, 1, 3, TH - 1, TH, 12]), (N, 8, 1, K)); zc[0] = rng.choice(np.array([TH, 12, 15]), (8, 1, K)); zc[1] = 1
    z = 255 * (1 - subset(rng, zc)); stk = endnames(rng); bas = endnames(rng); con = endnames(rng)
    for k in (0, K // 2, K - 1): z[1, 0, :, k] = 0
    ln = 1 + 14 * rng.integers(0, 2, (N, 8, K)); w = 1 + 256 * rng.integers(0, 2, (N, 8, 16, 1)); q = N - 1
    w[q, 7] = 257; w[q, 0] = 1; w[q, 6, 0] = 257; x[q, 6:8, :, 0] = 0; x[q, 7, :, W - 1] = 255; x[q, 6, :, W - 1] = 0; x[q, 6, 0, W - 1] = 255
    for k in (0, K - 1): stk[q, 7, :, k] = 0; stk[q, 7, 15, k] = W - 1
    for k in (1, K - 2): stk[q, 7, :, k] = W - 1
    for k in (2, K - 3): stk[q, 7, :, k] = 0; stk[q, 7, 0, k] = W - 1
    for k in (0, 1, 2, K - 3, K - 2, K - 1): z[q, 7, :, k] = 255
    for k in (2, K - 1): stk[q, 6, :, k] = W - 1; z[q, 6, :12, k] = 0; z[q, 6, 12:, k] = 255
    return pack(x, stk, bas, con, ln, z, w)
def setup_inputs_corners(rng):
    x, stk, bas, con, ln, z, w = parts(rng)
    cnt = rng.choice(np.array([0, TH - 1, TH, 16]), (N, 8, 1, W))
    over = rng.integers(0, 2, (N, 8, 1, W), dtype=np.int16) * rng.integers(0, 56, (N, 8, 16, W), dtype=np.int16)
    x = np.where(subset(rng, cnt) > 0, 200 + over, rng.integers(0, 200, (N, 8, 16, W), dtype=np.int16))
    z[:] = np.where(rng.random((N, 8, 1, K)) < 0.125, 201, 200); i = np.arange(16)[:, None]
    for q in range(N):
        for g in range(8):
            hot = np.flatnonzero(cnt[q, g, 0] >= TH); cold = np.flatnonzero(cnt[q, g, 0] < TH)
            row = rng.integers(1, 17, K); row[0] = 1; row[1] = 16; row[2] = 14; row[K - 1] = 15; row[K - 2] = 16
            hn = hot[rng.integers(0, len(hot), (16, K))]; cn = cold[rng.integers(0, len(cold), (16, K))]
            stk[q, g] = np.where(i == row, hn, np.where(i > row, stk[q, g], np.where((i == 0) & (rng.random((1, K)) < 0.5), hn, cn)))
    ln = rng.choice(np.array([1, 2, 14, 15]), (N, 8, K))
    for q in range(N): ln[q, q % 8] = 15; ln[q, (q + 1) % 8] = 1
    four = np.arange(K) % 4; stk[:, 3] = stk[:, 3][..., four]; z[:, 3] = z[:, 3][..., four]
    bas[:, 4] = (W - 1) * rng.integers(0, 2, (N, 16, K)); con[:, 2] = (W - 1) * rng.integers(0, 2, (N, 16, K))
    stk[:, 5] = stk[:, 5, :1].copy(); stk[:, 6] = E * np.arange(K) + rng.integers(0, E, (N, 16, K)); bas[:, 6] = E * np.arange(K) + rng.integers(0, E, (N, 16, K))
    w[0] = 1; w[N - 1] = 257
    return pack(x, stk, bas, con, ln, z, w)
def setup_inputs_long(rng):
    x, stk, bas, con, ln, z, w = parts(rng)
    x = np.where(rng.random((N, 8, 1, W)) < 0.06, rng.integers(250, 254, (N, 8, 16, W), dtype=np.int16), np.minimum(x, 249))
    ty = rng.random((N, 8, 1, K)); z = np.where(ty < 0.4, 250, np.where(ty < 0.8, 254, z)); ln = np.maximum(ln, rng.integers(1, 16, (N, 8, K)))
    return pack(x, stk, bas, con, ln, z, w)
def setup_inputs_alike(rng):
    x, stk, bas, con, ln, z, w = parts(rng); ga, gb, gc = [int(g) for g in rng.permutation(8)[:3]]; o = int(rng.integers(0, N))
    for a in (stk, bas, con):
        a[:, gb] = np.where(rng.random((N, 16, K)) < 0.5, E * rng.integers(K - 16, K, (N, 16, K)) + E - 1, a[:, gb])
    w[:, gb] = E * rng.integers(1, 256 // E + 1, (N, 16, 1)); w[:, gb, 0] = 1 + 256 * rng.integers(0, 2, (N, 1))
    for i in range(N):
        q = (o + i * ST) % N; lo, hi = ((32, 63), (96, 127), (192, 254), (96, 127), (0, 255))[min(i, 4)]
        if i < 4:
            x[q] = rng.integers(lo, hi + 1, (8, 16, W)); z[q] = 255 if i == 1 else 0
        if i == 2:
            m = np.zeros(8 * K, dtype=bool); m[rng.permutation(8 * K)[:K * int(rng.integers(0, 8)) + int(rng.integers(1, K))]] = True
            z[q] = np.where(m.reshape(8, 1, K), 255, 0)
        for g, v in ((ga, int(rng.integers(1, 4))), (gc, 0)):
            one = rng.integers(lo, hi - 2, 16); one[15] += (v - int(np.sum(one))) % 4
            x[q, g] = one[:, None]
        x[q, gb, 0] = (hi + 1) // E * E - 1
    return pack(x, stk, bas, con, ln, z, w)
def check_inputs(d):
    bad = []
    for k, lo, hi in (("xt", 0, 255), ("stk", 0, W - 1), ("bas", 0, W - 1), ("con", 0, W - 1), ("ln", 1, 15), ("z", 0, 255), ("w", 1, 257)):
        v = np.asarray(d[k]).astype(np.float32)
        if not (np.min(v) >= lo and np.max(v) <= hi and np.all(v == np.floor(v))): bad.append("range of " + k)
    return bad
def reference(xt, stk, bas, con, ln, z, w):
    X = xt.astype(np.float32).astype(np.int32).reshape(N, 8, 16, W); Z = z.astype(np.float32).astype(np.int64).reshape(N, 8, 16, K); wt = w.astype(np.int64).reshape(N, 8, 16, 1)
    S = stk.astype(np.int64).reshape(N, 8, 16, K); B = bas.astype(np.int64).reshape(N, 8, 16, K); C = con.astype(np.int64).reshape(N, 8, 16, K); n = ln.astype(np.int64).reshape(N, 8, K)
    A = [0] * N; p = np.arange(16)[None, :, None]
    for t in range(RO):
        for q in range(N):
            b = (q - t * ST) % N
            s, zz = S[b].copy(), Z[b].copy()
            R = np.take_along_axis(X[q], s.reshape(8, 1, 16 * K), 2).reshape(8, 16, 16, K).astype(np.int64)
            votes = np.add.reduce((R >= zz[:, :, None, :]).astype(np.int64), axis=1)
            hit = votes >= TH; hit[:, 0] = False
            found = np.maximum.accumulate(hit.astype(np.int64), axis=1)
            handled = found[:, 15] == 1; h = 16 - np.add.reduce(found, axis=1)
            M = np.max(np.where(found[:, None] == 1, 0, R), axis=2)
            u = np.add.reduce(wt[q] * M, axis=1) & 4095
            xh = np.take_along_axis(R, np.minimum(h, 15)[:, None, None, :], 2)[:, :, 0]
            v = np.add.reduce(xh, axis=1) & 3
            j = (((u * u) >> 5) + u + A[q]) & (K - 1)
            paste = handled & (v > 0)
            m = np.where(paste, np.take_along_axis(n[q], j, 1), 0)
            src = p + (np.where(paste, h + 1, h) - m)[:, None, :]
            low = np.take_along_axis(s, np.clip(src, 0, 15), 1); piece = np.take_along_axis(C[q], j[:, None, :], 2)
            new = np.where(p < m[:, None, :], piece, np.where(src <= 15, low, B[b]))
            S[b] = np.where(handled[:, None, :], new, s)
            Z[b] = np.where(handled[:, None, :], np.abs(xh - zz), M)
            C[q] = np.where(paste[:, None, :] & (p < h[:, None, :]), s, C[q])
            n[q] = np.where(paste, h, n[q])
            A[q] = int(np.sum(np.where(handled, 0, 1)))
            if t < RO - 1:
                col = (E * np.arange(K) + (u & (E - 1)))[:, None, :]
                np.put_along_axis(X[q], col, ((np.take_along_axis(X[q], col, 2) + M) >> 1).astype(np.int32), 2)
    last = [(q - (RO - 1) * ST) % N for q in range(N)]
    return {"ys": S[last].reshape(N, 128, K).astype(np.float32), "yc": C.reshape(N, 128, K).astype(np.float32), "yn": n.astype(np.float32), "yz": Z[last].reshape(N, 128, K).astype(np.float32).astype(BF)}

@@ -1,0 +1,419 @@
+from concourse.mybir import AluOpType, AxisListType, ActivationFunctionType
+
+ROUNDS, STEP, K, NREC = 3, 3, 512, 8192
+CHUNKS = [(0, 128), (128, 256), (256, 384), (384, 448), (448, 512)]
+NP = 1 << 20
+TOP = 1 << 22
+
+SCRATCH = {
+    "X": ("sbuf", [128, NREC], "bfloat16"),
+    "RP": ("sbuf", [128, 2 * NREC], "bfloat16"),
+    "GE": ("sbuf", [128, 32, 256], "bfloat16"),
+    "Y": ("sbuf", [128, 16 * K], "int32"),
+    "D": ("dram", [8, 32, K], "int32"),
+    "STK": ("sbuf", [128, K], "int32"), "CON": ("sbuf", [128, K], "int32"),
+    "LN8": ("sbuf", [128, K], "int32"), "LNB": ("sbuf", [128, K], "bfloat16"), "LX": ("sbuf", [128, K], "float32"),
+    "WI": ("sbuf", [128, 1], "int32"), "WF": ("sbuf", [128, 1], "float32"),
+    "CM0": ("sbuf", [128, 1040], "float32"), "CM1": ("sbuf", [128, 1040], "float32"),
+    "LW0": ("sbuf", [128, 560], "bfloat16"), "LW1": ("sbuf", [128, 560], "bfloat16"),
+    "CF0": ("sbuf", [128, K], "float32"), "CF1": ("sbuf", [128, K], "float32"), "CFI": ("sbuf", [128, K], "int32"),
+    "M16": ("sbuf", [128, K], "float16"), "AG": ("sbuf", [128, K], "bfloat16"), "ZZ": ("sbuf", [128, K], "bfloat16"),
+    "OX": ("sbuf", [128, K], "bfloat16"), "NR": ("sbuf", [128, K], "int32"),
+    "T1": ("sbuf", [128, K], "bfloat16"), "OA": ("sbuf", [128, K], "float32"), "OB": ("sbuf", [128, K], "float32"),
+    "LM": ("sbuf", [128, K], "bfloat16"), "LS": ("sbuf", [128, K], "bfloat16"),
+    "BE": ("sbuf", [128, K], "float32"), "PB": ("sbuf", [128, K], "float32"), "TY": ("sbuf", [128, K], "int32"),
+    "SN": ("sbuf", [128, K], "int32"), "FO": ("sbuf", [128, K], "float32"), "FC": ("sbuf", [128, K], "float32"),
+    "FN": ("sbuf", [128, K], "float32"),
+    "E": ("sbuf", [128, K], "float32"), "ONE": ("sbuf", [128, K], "float32"), "KC": ("sbuf", [128, 1], "float32"),
+    "RC": ("sbuf", [128, 1], "float32"), "IC": ("sbuf", [128, 1], "float32"),
+    "TA": ("sbuf", [128, 128], "float32"), "TB": ("sbuf", [128, 128], "float32"),
+    "ID": ("sbuf", [128, 128], "bfloat16"), "ND": ("sbuf", [128, 128], "bfloat16"), "IH": ("sbuf", [128, 128], "float16"),
+    "BQ": ("sbuf", [128, 144], "bfloat16"), "BW": ("sbuf", [128, 144], "float16"),
+    "GA": ("sbuf", [128, 128], "bfloat16"),
+    "DG": ("sbuf", [128, K], "bfloat16"), "MK": ("sbuf", [128, 2048], "bfloat16"),
+    "D1A": ("sbuf", [128, K], "float32"), "D1B": ("sbuf", [128, K], "float32"),
+    "KW": ("sbuf", [128, 32], "float32"), "K16": ("sbuf", [128, 32], "float32"), "KH": ("sbuf", [128, 32], "float32"),
+    "K5": ("sbuf", [128, 32], "float32"), "KI": ("sbuf", [128, 32], "float32"),
+    "LB": ("sbuf", [128, 64], "float32"), "L2": ("sbuf", [128, 192], "float32"), "L2S": ("sbuf", [128, 192], "float32"),
+    "L2T": ("sbuf", [128, 192], "float32"),
+    "ACOL": ("sbuf", [128, 1], "float32"), "RED": ("sbuf", [128, 1], "float32"),
+    "ZP": ("psum", [128, K], "float32"), "UU": ("psum", [128, K], "float32"), "VV": ("psum", [128, K], "float32"),
+    "PX": ("psum", [128, K], "float32"),
+}
+for _n in range(4):
+    SCRATCH["VT%d" % _n] = ("psum", [128, K], "float32")
+for _t in range(3):
+    SCRATCH["SU%d" % _t] = ("sbuf", [128, K], "uint16")
+    SCRATCH["SE%d" % _t] = ("sbuf", [128, K], "int32")
+    SCRATCH["Z%d" % _t] = ("sbuf", [128, 528], "bfloat16")
+    SCRATCH["BA%d" % _t] = ("sbuf", [128, K], "int32")
+    SCRATCH["ZO%d" % _t] = ("sbuf", [128, K], "bfloat16")
+    if _t < 2:
+        SCRATCH["UO%d" % _t] = ("sbuf", [128, K], "uint16")
+        SCRATCH["EO%d" % _t] = ("sbuf", [128, K], "int32")
+WF32 = ["h", "un", "u20", "zq", "zl", "h5", "h1k", "np0", "np", "w0", "w1", "n32", "hl", "p5", "cl", "pz", "h528", "lp", "ll"]
+WI32 = ["vi", "v", "ui", "u", "u2", "q", "j0", "j", "d", "dd", "x15", "xk"]
+WU16 = ["MLu", "ALu", "zlu", "jlu", "hlu", "ylu", "xlu", "clu", "llu"]
+SCRATCH["FW"] = ("sbuf", [128, 32 * len(WF32)], "float32")
+SCRATCH["IW"] = ("sbuf", [128, 32 * len(WI32)], "int32")
+SCRATCH["LU"] = ("sbuf", [128, 32 * len(WU16)], "uint16")
+TILE = {}
+for _i, _n in enumerate(WF32): TILE["f_" + _n] = ("FW", 32 * _i)
+for _i, _n in enumerate(WI32): TILE["i_" + _n] = ("IW", 32 * _i)
+for _i, _n in enumerate(WU16): TILE[_n] = ("LU", 32 * _i)
+
+LOADS = ["STK", "X", "Z0", "WI", "LN8", "BA0", "CON"]
+ARR = ["SU1", "SU2", "SE1", "SE2", "Z1", "Z2", "BA1", "BA2"]
+SEMAPHORES = (["sV", "sA", "sP", "sG", "local", "dD", "dY", "oS", "oZ", "oC", "oN"]
+              + ["ld" + n for n in LOADS] + ["ar" + n for n in ARR])
+
+
+def rank_program(g, core, T, topo):
+    rank = T.rank_of(core)
+    if rank is None:
+        return
+    op = AluOpType
+    act = ActivationFunctionType
+    queue = {"V": g.vector, "A": g.scalar, "P": g.tensor, "G": g, "S": g.sync}
+    total = {s: 0 for s in SEMAPHORES}
+    seen = {q: {} for q in queue}
+    snap = {}
+    hist = {}
+
+    def learn(q, sem, cnt):
+        if seen[q].get(sem, 0) < cnt: seen[q][sem] = cnt
+        for s, n in snap.get((sem, cnt), {}).items():
+            if seen[q].get(s, 0) < n: seen[q][s] = n
+
+    def await_deps(q, reads, writes, own_waw):
+        need = {}
+        for lst, isw in ((reads, False), (writes, True)):
+            for name, lo, hi in lst:
+                ps = SCRATCH.get(name, ("", 0, 0))[0] == "psum"
+                for l, h, w, oq, sem, cnt in hist.get(name, []):
+                    if not ps and (h <= lo or hi <= l): continue
+                    if oq == q:
+                        if not (w and (not isw or own_waw)): continue
+                    elif not (isw or w or ps): continue
+                    if sem[0] in "ldo": cnt = total[sem]
+                    if need.get(sem, 0) < cnt: need[sem] = cnt
+        for sem in sorted(need, key=lambda s: -need[s]):
+            if seen[q].get(sem, 0) < need[sem]:
+                queue[q].wait_ge(T.sem[sem], need[sem])
+                learn(q, sem, need[sem])
+
+    def note(oq, q, reads, writes, sem, cnt):
+        snap[(sem, cnt)] = dict(seen[q]) if q else {}
+        for name, lo, hi in writes:
+            old = [e for e in hist.get(name, []) if not (lo <= e[0] and e[1] <= hi)]
+            hist[name] = old + [(lo, hi, True, oq, sem, cnt)]
+        for name, lo, hi in reads:
+            old = [e for e in hist.get(name, []) if not (not e[2] and e[3] == oq and lo <= e[0] and e[1] <= hi)]
+            hist[name] = old + [(lo, hi, False, oq, sem, cnt)]
+
+    def run(q, fn, out, ins, own_waw=False):
+        reads = [x for i in ins for x in i[1]]
+        writes = list(out[1])
+        for x in out[2:]: reads += x
+        await_deps(q, reads, writes, own_waw)
+        sem = "s" + q
+        total[sem] += 1
+        fn().then_inc(T.sem[sem], 1)
+        note(q, q, reads, writes, sem, total[sem])
+
+    def dma(q, out, in_, sem, last=True):
+        await_deps(q, in_[1], out[1], True)
+        total[sem] += 16
+        queue[q].dma_start(out[0], in_[0]).then_inc(T.sem[sem], 16)
+        note("dma" + sem, q, in_[1], out[1], sem, total[sem])
+
+    def b(name, lo=0, hi=None, step=1, p0=0, p1=128):
+        if name in TILE:
+            name, o = TILE[name]
+            lo, hi = o + lo, o + (32 if hi is None else hi)
+        hi = SCRATCH[name][1][-1] if hi is None else hi
+        ap = T[name][p0:p1, lo:hi] if step == 1 else T[name][p0:p1, lo:hi:step]
+        return (ap, [(name, lo, hi)])
+
+    def ind(name, lo, hi, lst, c0=0, c1=32):
+        lst, o = TILE.get(lst, (lst, 0))
+        return (T[name][:, lo:hi].indirect(T[lst][:, o + c0:o + c1]), [(name, lo, hi), (lst, o + c0, o + c1)])
+
+    def tt(out, a, c, o):
+        run("V", lambda: g.vector.tensor_tensor(out[0], a[0], c[0], o), out, [a, c])
+
+    def ts(out, a, s1, o1, s2=None, o2=None, waw=False):
+        ins = [a] + ([s1] if isinstance(s1, tuple) else [])
+        v1 = s1[0] if isinstance(s1, tuple) else s1
+        if o2 is None:
+            run("V", lambda: g.vector.tensor_scalar(out[0], a[0], v1, None, o1), out, ins, waw)
+        else:
+            run("V", lambda: g.vector.tensor_scalar(out[0], a[0], v1, s2, o1, o2), out, ins, waw)
+
+    def cp(out, a, waw=False):
+        run("V", lambda: g.vector.tensor_copy(out[0], a[0]), out, [a], waw)
+
+    def scan(out, a, c, o1, o2):
+        run("V", lambda: g.vector.tensor_tensor_scan(out[0], a[0], c[0], 0.0, o1, o2), out, [a, c])
+
+    def fill(out, v, waw=False):
+        run("V", lambda: g.vector.memset(out[0], v), out, [], waw)
+
+    def ac(out, a, func=act.Copy, scale=1.0):
+        if scale == 1.0:
+            run("A", lambda: g.scalar.activation(out[0], a[0], func), out, [a])
+        else:
+            run("A", lambda: g.scalar.activation(out[0], a[0], func, scale=scale), out, [a])
+
+    def mm(out, l, r, start, stop):
+        run("P", lambda: g.tensor.matmul(out[0], l[0], r[0], start, stop), out, [l, r])
+
+    def iota(out, pattern, base, cm):
+        run("G", lambda: g.iota(out[0], pattern, base, cm, allow_small_or_imprecise_dtypes=True), out, [])
+
+    def select(out, a, pattern, cmp, fillv, base, cm):
+        run("G", lambda: g.affine_select(out[0], a[0], pattern, cmp, fillv, base, cm), out, [a])
+
+    def send(src, dst_name, lo, hi, dst):
+        await_deps("G", src[1], [], False)
+        rid, pid, _se = topo.addr(dst)
+        m = topo.mask(core, dst)
+        n = len(topo.engines(core, dst))
+        g.remote_dma(T[dst_name][:, lo:hi], src[0], T.sem["ar" + dst_name], T.sem["local"], pid, rid, m)
+        total["local"] += n
+
+    def arrives(name, lo, hi, src):
+        n = len(topo.engines(src, core))
+        total["ar" + name] += n
+        note("remote", None, [], [(name, lo, hi)], "ar" + name, n)
+
+    nxt = T.cores[(rank + STEP) % len(T.cores)]
+    nxt2 = T.cores[(rank + 2 * STEP) % len(T.cores)]
+    prv = T.cores[(rank - STEP) % len(T.cores)]
+    prv2 = T.cores[(rank - 2 * STEP) % len(T.cores)]
+    for n in ("SU", "SE"):
+        for t in (1, 2): arrives("%s%d" % (n, t), 0, K, prv)
+    for t in (1, 2): arrives("Z%d" % t, 0, K, prv)
+    arrives("BA1", 0, K, prv)
+    arrives("BA2", 0, K, prv2)
+
+    dma("S", b("STK"), (T.stk[:, :], []), "ldSTK")
+    dma("S", b("X"), (T.xt[:, :], []), "ldX")
+    dma("A", b("WI"), (T.w[:, :], []), "ldWI")
+    dma("A", b("LN8", p1=8), (T.ln[:, :], []), "ldLN8")
+    dma("A", b("Z0", 0, K), (T.z[:, :], []), "ldZ0")
+    dma("A", b("BA0"), (T.bas[:, :], []), "ldBA0")
+    dma("A", b("CON"), (T.con[:, :], []), "ldCON")
+
+    fill(b("ONE"), 1.0)
+    select(b("E", p1=16), b("ONE", p1=16), [[0, 32], [-1, 16]], op.is_equal, 0.0, 0, 1)
+    iota(b("KC", p1=16), [[0, 1]], 0, 1)
+    mm(b("PX", 0, 1), b("E", 0, 128, p1=16), b("KC", p1=16), True, True)
+    cp(b("RC"), b("PX", 0, 1))
+    ts(b("IC"), b("RC"), 16384.0, op.mult)
+    ts(b("SE0"), b("STK"), b("IC"), op.add)
+    cp(b("SU0"), b("STK"))
+
+    def rotations(t):
+        se = b("SE%d" % t)
+        for half in (0, 1):
+            dma("S", (T.D[:, 16 * half:16 * half + 16, :], [("D", 16 * half, 16 * half + 16)]), se, "dD")
+        for q in range(16):
+            dma("S", (T.Y[q::16, :], [("Y", q * 100000, q * 100000 + 1)]), (T.D[:, q:q + 16, :], [("D", q, q + 16)]), "dY")
+
+    yall = [("Y", 0, 1600000)]
+    rotations(0)
+
+    select(b("TA"), b("ONE", 0, 128), [[-1, 128]], op.is_equal, 0.0, 0, 1)
+    cp(b("ID"), b("TA"))
+    ts(b("ND"), b("TA"), -1.0, op.mult)
+    cp(b("IH"), b("TA"))
+    mm(b("PX"), b("E", 0, 128, p1=16), b("E", p1=16), True, True)
+    cp(b("DG"), b("PX"))
+    select(b("TB", 0, 9), b("ONE", 0, 9), [[-16, 9]], op.is_ge, 0.0, 0, 1)
+    select(b("TB", 16, 25), b("TB", 0, 9), [[16, 9]], op.is_ge, 0.0, 15, -1)
+    fill(b("BQ"), 0.0)
+    cp(b("BQ", 15, 144, 16), b("TB", 16, 25), True)
+    cp(b("WF"), b("WI"))
+    ts(b("BW"), b("BQ"), b("WF"), op.mult)
+    fill(b("MK"), 1.0)
+    fill(b("MK", 0, 2048, 16), 0.0, True)
+    fill((T.GE[:, :, 0:256:16], [("GE", 0, 8192)]), 1.0)
+    iota(b("KI"), [[16, 32]], 0, 0)
+    ts(b("KW"), b("KI"), b("RC"), op.add)
+    ts(b("K16"), b("KW"), 16.0, op.mult)
+    ts(b("K5"), b("KW"), 512.0, op.add)
+    fill(b("D1A"), -1.0)
+    fill(b("D1B"), -1.0)
+    fill(b("D1A", 0, K, 16), 15.0, True)
+    for l0, l1 in CHUNKS:
+        n, c0, c1 = l1 - l0, l0 // 16, l1 // 16
+        ts(b("KH", c0, c1), b("K16", c0, c1), float(16 * n - 1 - 16 * l0), op.add)
+        ts(b("D1A", l0 + 15, l1, 16), b("K16", c0, c1), float(16 * n + 14 - 16 * l0), op.add, waw=True)
+        fill(b("D1B", l0, l1, 16), float(16 * n + 14), True)
+        ts(b("D1B", l0 + 15, l1, 16), b("K16", c0, c1), float(15 - 16 * l0), op.add, waw=True)
+    for t in range(3): fill(b("Z%d" % t, K, 528), 0.0)
+    iota(b("LB", 0, 32), [[16384, 32]], 8192, 0)
+    iota(b("LB", 32, 64), [[16384, 32]], -8192, 0)
+    fill(b("LB", 48, 64), -1048576.0, True)
+    for t in range(3): fill(b("L2S", 64 * t, 64 * t + 64, p1=16), float(TOP + (t + 1) * NP))
+    for t in range(3):
+        select(b("L2T", 64 * t, 64 * t + 64, p1=16), b("L2S", 64 * t, 64 * t + 64, p1=16), [[1, 64]], op.is_ge, -float(TOP), -1, -1)
+    mm(b("PX", 0, 192), b("E", 0, 128, p1=16), b("L2T", p1=16), True, True)
+    cp(b("L2"), b("PX", 0, 192))
+    select(b("TA", p1=8), b("ONE", 0, 128, p1=8), [[1, 128]], op.is_ge, 0.0, 0, -16)
+    select(b("TB", p1=8), b("TA", p1=8), [[-1, 128]], op.is_ge, 0.0, 15, 16)
+    cp(b("GA", p1=8), b("TB", p1=8))
+    cp(b("LNB", p1=8), b("LN8", p1=8))
+    mm(b("PX"), b("GA", p1=8), b("LNB", p1=8), True, True)
+    ac(b("LW0", 0, K), b("PX"), scale=512.0)
+    ts(b("LX"), b("PX"), b("RC"), op.is_gt, float(TOP), op.mult)
+    tt(b("CM0", 0, K), b("LX"), b("CON"), op.add)
+    for n in ("LW0", "LW1"):
+        fill(b(n, 512, 528), 512.0)
+        iota(b(n, 528, 560), [[512, 32]], 0, 0)
+    for n in ("CM0", "CM1"): fill(b(n, 512, 528), -1.0)
+
+    send(b("BA0"), "BA1", 0, K, nxt)
+    send(b("BA0"), "BA2", 0, K, nxt2)
+
+    for t in range(ROUNDS):
+        last = t == ROUNDS - 1
+        SU, SE, Z, BA = "SU%d" % t, "SE%d" % t, "Z%d" % t, "BA%d" % t
+        CMc, CMn = "CM%d" % (t % 2), "CM%d" % ((t + 1) % 2)
+        LWc, LWn = "LW%d" % (t % 2), "LW%d" % ((t + 1) % 2)
+        if t: rotations(t)
+        mm(b("ZP"), b("ID"), b(Z, 0, K), True, True)
+
+        def records(ci):
+            l0, l1 = CHUNKS[ci]
+            ac(b("RP", 32 * l0, 32 * l0 + 16 * (l1 - l0)), ind("X", 0, NREC, SU, l0, l1))
+
+        def compare(ci):
+            l0, l1 = CHUNKS[ci]
+            c0, c1, a0, n = l0 // 16, l1 // 16, 32 * l0, 16 * (l1 - l0)
+            for i in range(1, 16):
+                tt((T.GE[:, c0:c1, i:256:16], [("GE", 256 * c0, 256 * c1)]), (T.RP[:, a0 + i:a0 + n:16], [("RP", a0, a0 + n)]),
+                   b("ZP", l0, l1), op.is_ge)
+            scan(b("RP", a0 + n, a0 + 2 * n), b("MK", 0, n), b("RP", a0, a0 + n), op.mult, op.max)
+
+        def votes(ci):
+            l0, l1 = CHUNKS[ci]
+            c0, c1 = l0 // 16, l1 // 16
+            for r in range(16):
+                mm(b("VT%d" % (ci % 4), 0, l1 - l0), b("BQ", 15 - r, 143 - r),
+                   (T.GE[:, c0:c1, 16 * r:16 * r + 16], [("GE", 256 * c0, 256 * c1)]), r == 0, r == 15)
+
+        def handler(ci):
+            l0, l1 = CHUNKS[ci]
+            c0, c1 = l0 // 16, l1 // 16
+            ts(b("T1", l0, l1), b("VT%d" % (ci % 4), 0, l1 - l0), 8.0, op.is_lt, 32768.0, op.mult)
+            scan(b("OA", l0, l1), b("T1", l0, l1), b("D1A", l0, l1), op.min, op.add)
+            scan(b("OB", l0, l1), b("T1", l0, l1), b("D1B", l0, l1), op.min, op.add)
+            cp(b("MLu", c0, c1), b("OA", l0 + 15, l1, 16))
+            cp(b("ALu", c0, c1), b("OB", l0 + 15, l1, 16))
+            cp(b("M16", l0, l1), ind("RP", 32 * l0, 32 * l1, "MLu", c0, c1))
+
+        def taken(ci):
+            l0, l1 = CHUNKS[ci]
+            ac(b("AG", l0, l1), ind("RP", 32 * l0, 32 * l1, "ALu", l0 // 16, l1 // 16))
+
+        for ci in range(3): records(ci)
+        for ci in range(5):
+            compare(ci)
+            votes(ci)
+            if ci:
+                handler(ci - 1)
+                if ci + 2 < 5: records(ci + 2)
+                taken(ci - 1)
+        handler(4)
+        taken(4)
+        for r in range(16): mm(b("UU", 0, 32), b("BW", 15 - r, 143 - r), b("M16", r, K, 16), r == 0, r == 15)
+        for r in range(16): mm(b("VV", 0, 32), b("BQ", 15 - r, 143 - r), b("AG", r, K, 16), r == 0, r == 15)
+
+        w = lambda n: b("f_" + n)
+        x = lambda n: b("i_" + n)
+        tt(w("h"), b("OA", 15, K, 16), b("KH"), op.subtract)
+        ts(w("zq"), w("h"), 16.0, op.is_ge, 512.0, op.mult)
+        ts(w("u20"), w("h"), 16.0, op.is_ge, float(NP), op.mult)
+        tt(w("zl"), w("zq"), b("KW"), op.max)
+        ts(w("h5"), w("h"), 512.0, op.mult)
+        cp(b("zlu"), w("zl"))
+        tt(w("h1k"), w("h5"), b("K5"), op.add)
+        cp(x("ui"), b("UU", 0, 32))
+        ts(x("u"), x("ui"), 4095, op.bitwise_and)
+        tt(x("u2"), x("u"), x("u"), op.mult)
+        cp(x("vi"), b("VV", 0, 32))
+        ts(x("q"), x("u2"), 5, op.arith_shift_right)
+        ts(x("v"), x("vi"), 3, op.bitwise_and)
+        if t: ts(w("w0"), x("u"), b("ACOL"), op.add)
+        ts(w("np0"), x("v"), 0.0, op.is_equal, float(NP), op.mult)
+        tt(w("np"), w("np0"), w("u20"), op.max)
+        tt(w("w1"), w("w0") if t else x("u"), w("np"), op.add)
+        tt(x("j0"), x("q"), w("w1"), op.add)
+        if not last: ts(x("x15"), x("u"), 15, op.bitwise_and)
+        ts(x("j"), x("j0"), NP + 511, op.bitwise_and)
+        if not last: tt(x("xk"), x("x15"), b("K16"), op.add)
+        ts(b("jlu"), x("j"), 512.0, op.min)
+        ts(w("n32"), w("np"), 1.0 / 32768.0, op.mult)
+        tt(b("LM"), ind(LWc, 0, 528, "jlu"), b("DG"), op.mult)
+        if not last: cp(b("xlu"), x("xk"))
+        tt(w("hl"), w("n32"), w("h"), op.add)
+        scan(b("LS"), b("MK", 0, K), b("LM"), op.mult, op.add)
+        cp(b("hlu"), w("hl"))
+        tt(x("d"), w("h1k"), b("LS", 15, K, 16), op.subtract)
+        tt(b("BE"), ind("LB", 0, 64, "hlu"), b(BA), op.add)
+        ts(x("dd"), x("d"), 8191, op.bitwise_and)
+        tt(b("PB"), ind(CMc, 0, 528, "jlu"), b("BE"), op.max)
+        cp(b("ylu"), x("dd"))
+        ac(b("ZZ"), ind(Z, 0, 528, "zlu"))
+        mm(b("VT3"), b("ID"), b("AG"), True, False)
+        mm(b("VT3"), b("ND"), b("ZZ"), False, True)
+        if not last:
+            ac(b("OX"), ind("X", 0, NREC, "xlu"))
+            mm(b("VT2"), b("IH"), b("M16"), True, False)
+            mm(b("VT2"), b("ID"), b("OX"), False, True)
+        ac(b("ZO%d" % t), b("VT3"), act.Abs)
+        yi = ind("Y", 0, 16 * K, "ylu")
+        tt(b("TY"), (yi[0], yall + yi[1][1:]), b("PB"), op.max)
+        ts(b("SN"), b("TY"), 8191, op.bitwise_and)
+        if not last:
+            cp(b("UO%d" % t), b("SN"))
+            ts(b("EO%d" % t), b("SN"), b("IC"), op.add)
+            send(b("ZO%d" % t), "Z%d" % (t + 1), 0, K, nxt)
+            send(b("UO%d" % t), "SU%d" % (t + 1), 0, K, nxt)
+            send(b("EO%d" % t), "SE%d" % (t + 1), 0, K, nxt)
+            ts(b("NR"), b("VT2"), 0.5, op.mult, -0.25, op.add)
+            si = ind("X", 0, NREC, "xlu")
+            cp((si[0], si[1][:1], si[1][1:]), b("NR"))
+        else:
+            cp(b("FO"), b("SN"))
+            dma("S", (T.ys[:, :], []), b("FO"), "oS")
+            dma("S", (T.yz[:, :], []), b("ZO%d" % t), "oZ")
+        tt(b(CMc, 528, 1040), ind("L2", 64 * t, 64 * t + 64, "hlu"), b(SE), op.add)
+        ts(w("p5"), w("np"), 1.0, op.is_lt, 528.0, op.mult)
+        ts(w("pz"), w("np"), 1.0, op.is_lt)
+        ts(w("h528"), w("h"), 528.0, op.add)
+        tt(w("cl"), w("p5"), b("KW"), op.add)
+        tt(w("lp"), w("h528"), w("pz"), op.mult)
+        cp(b("clu"), w("cl"))
+        tt(w("ll"), w("lp"), b("KW"), op.max)
+        cf_old = b("CON") if t == 0 else b("CF%d" % ((t + 1) % 2))
+        tt(b("CFI") if last else b("CF%d" % (t % 2)), ind(CMc, 0, 1040, "clu"), cf_old, op.max)
+        cp(b("llu"), w("ll"))
+        ac(b(LWn, 0, K), ind(LWc, 0, 560, "llu"))
+        if not last:
+            ac(b(CMn, 0, K), ind(CMc, 0, 1040, "clu"))
+            ts(w("un"), w("h"), 16.0, op.is_ge)
+            run("V", lambda: g.vector.tensor_reduce(T.RED[:, :], w("un")[0], AxisListType.X, op.add), b("RED"), [w("un")])
+            mm(b("PX", 0, 1), b("ONE", 0, 128), b("RED"), True, True)
+            cp(b("ACOL"), b("PX", 0, 1))
+        else:
+            ts(b("TY"), b("CFI"), 8191, op.bitwise_and)
+            cp(b("FC"), b("TY"))
+            dma("S", (T.yc[:, :], []), b("FC"), "oC")
+            ac(b("FN"), b(LWn, 0, K), scale=1.0 / 512.0)
+            dma("S", (T.yn[:, :], []), (T.FN[0:128:16, :], [("FN", 0, K)]), "oN")
+
+    for s in SEMAPHORES:
+        if total[s]: g.wait_ge(T.sem[s], total[s])

@@ -1,9 +1,12 @@
 from concourse.mybir import AluOpType, AxisListType, ActivationFunctionType
 
 ROUNDS, STEP, K, NREC = 3, 3, 512, 8192
-CHUNKS = [(0, 128), (128, 256), (256, 384), (384, 448), (448, 512)]
+EDGES = [0, 64, 192, 320, 448, 512]
+CHUNKS = list(zip(EDGES[:-1], EDGES[1:]))
+LATER = 2
 NP = 1 << 20
 TOP = 1 << 22
+WHOLE = 12582912.0
 
 SCRATCH = {
     "X": ("sbuf", [128, NREC], "bfloat16"),
@@ -17,31 +20,32 @@ SCRATCH = {
     "CM0": ("sbuf", [128, 1040], "float32"), "CM1": ("sbuf", [128, 1040], "float32"),
     "LW0": ("sbuf", [128, 560], "bfloat16"), "LW1": ("sbuf", [128, 560], "bfloat16"),
     "CF0": ("sbuf", [128, K], "float32"), "CF1": ("sbuf", [128, K], "float32"), "CFI": ("sbuf", [128, K], "int32"),
-    "M16": ("sbuf", [128, K], "float16"), "AG": ("sbuf", [128, K], "bfloat16"), "ZZ": ("sbuf", [128, K], "bfloat16"),
-    "OX": ("sbuf", [128, K], "bfloat16"), "NR": ("sbuf", [128, K], "int32"),
+    "MB": ("sbuf", [128, K], "bfloat16"), "AG": ("sbuf", [128, K], "bfloat16"), "ZZ": ("sbuf", [128, K], "bfloat16"),
+    "OX": ("sbuf", [128, K], "bfloat16"), "NF": ("sbuf", [128, K], "float32"), "NB": ("sbuf", [128, K], "bfloat16"),
     "T1": ("sbuf", [128, K], "bfloat16"), "OA": ("sbuf", [128, K], "float32"), "OB": ("sbuf", [128, K], "float32"),
-    "LM": ("sbuf", [128, K], "bfloat16"), "LS": ("sbuf", [128, K], "bfloat16"),
+    "LG": ("sbuf", [128, K], "bfloat16"),
     "BE": ("sbuf", [128, K], "float32"), "PB": ("sbuf", [128, K], "float32"), "TY": ("sbuf", [128, K], "int32"),
     "SN": ("sbuf", [128, K], "int32"), "FO": ("sbuf", [128, K], "float32"), "FC": ("sbuf", [128, K], "float32"),
-    "FN": ("sbuf", [128, K], "float32"),
-    "E": ("sbuf", [128, K], "float32"), "ONE": ("sbuf", [128, K], "float32"), "KC": ("sbuf", [128, 1], "float32"),
+    "FI": ("sbuf", [128, K], "int32"), "FN": ("sbuf", [128, K], "float32"),
+    "E": ("sbuf", [128, K], "float32"), "ONE": ("sbuf", [128, 128], "float32"), "ON16": ("sbuf", [128, K], "float32"),
+    "KC": ("sbuf", [128, 1], "float32"),
     "RC": ("sbuf", [128, 1], "float32"), "IC": ("sbuf", [128, 1], "float32"),
-    "TA": ("sbuf", [128, 128], "float32"), "TB": ("sbuf", [128, 128], "float32"),
-    "ID": ("sbuf", [128, 128], "bfloat16"), "ND": ("sbuf", [128, 128], "bfloat16"), "IH": ("sbuf", [128, 128], "float16"),
+    "TA": ("sbuf", [128, 128], "float32"), "TB": ("sbuf", [128, 32], "float32"),
+    "TC": ("sbuf", [128, 128], "float32"), "TD": ("sbuf", [128, 128], "float32"),
+    "ID": ("sbuf", [128, 128], "bfloat16"), "ND": ("sbuf", [128, 128], "bfloat16"), "HI": ("sbuf", [128, 128], "bfloat16"),
+    "HQ": ("sbuf", [128, 128], "bfloat16"), "ONB": ("sbuf", [128, K], "bfloat16"),
     "BQ": ("sbuf", [128, 144], "bfloat16"), "BW": ("sbuf", [128, 144], "float16"),
-    "GA": ("sbuf", [128, 128], "bfloat16"),
-    "DG": ("sbuf", [128, K], "bfloat16"), "MK": ("sbuf", [128, 2048], "bfloat16"),
+    "GA": ("sbuf", [128, 128], "bfloat16"), "MK": ("sbuf", [128, 2048], "bfloat16"),
     "D1A": ("sbuf", [128, K], "float32"), "D1B": ("sbuf", [128, K], "float32"),
     "KW": ("sbuf", [128, 32], "float32"), "K16": ("sbuf", [128, 32], "float32"), "KH": ("sbuf", [128, 32], "float32"),
     "K5": ("sbuf", [128, 32], "float32"), "KI": ("sbuf", [128, 32], "float32"),
     "LB": ("sbuf", [128, 64], "float32"), "L2": ("sbuf", [128, 192], "float32"), "L2S": ("sbuf", [128, 192], "float32"),
     "L2T": ("sbuf", [128, 192], "float32"),
     "ACOL": ("sbuf", [128, 1], "float32"), "RED": ("sbuf", [128, 1], "float32"),
-    "ZP": ("psum", [128, K], "float32"), "UU": ("psum", [128, K], "float32"), "VV": ("psum", [128, K], "float32"),
-    "PX": ("psum", [128, K], "float32"),
 }
-for _n in range(4):
-    SCRATCH["VT%d" % _n] = ("psum", [128, K], "float32")
+BANKS = ["ZP", "UU", "VV", "PX", "VT0", "VT1", "DF0", "DF1"]
+for _n in BANKS:
+    SCRATCH[_n] = ("psum", [128, K], "float32")
 for _t in range(3):
     SCRATCH["SU%d" % _t] = ("sbuf", [128, K], "uint16")
     SCRATCH["SE%d" % _t] = ("sbuf", [128, K], "int32")
@@ -53,7 +57,7 @@ for _t in range(3):
         SCRATCH["EO%d" % _t] = ("sbuf", [128, K], "int32")
 WF32 = ["h", "un", "u20", "zq", "zl", "h5", "h1k", "np0", "np", "w0", "w1", "n32", "hl", "p5", "cl", "pz", "h528", "lp", "ll"]
 WI32 = ["vi", "v", "ui", "u", "u2", "q", "j0", "j", "d", "dd", "x15", "xk"]
-WU16 = ["MLu", "ALu", "zlu", "jlu", "hlu", "ylu", "xlu", "clu", "llu"]
+WU16 = ["MLu", "ALu", "zlu", "jlu", "hlu", "ylu", "xlu", "clu", "llu", "huu"]
 SCRATCH["FW"] = ("sbuf", [128, 32 * len(WF32)], "float32")
 SCRATCH["IW"] = ("sbuf", [128, 32 * len(WI32)], "int32")
 SCRATCH["LU"] = ("sbuf", [128, 32 * len(WU16)], "uint16")
@@ -89,12 +93,13 @@ def rank_program(g, core, T, topo):
         need = {}
         for lst, isw in ((reads, False), (writes, True)):
             for name, lo, hi in lst:
-                ps = SCRATCH.get(name, ("", 0, 0))[0] == "psum"
+                ps = name in BANKS
                 for l, h, w, oq, sem, cnt in hist.get(name, []):
                     if not ps and (h <= lo or hi <= l): continue
                     if oq == q:
                         if not (w and (not isw or own_waw)): continue
                     elif not (isw or w or ps): continue
+                    if seen[q].get(sem, 0) >= cnt: continue
                     if sem[0] in "ldo": cnt = total[sem]
                     if need.get(sem, 0) < cnt: need[sem] = cnt
         for sem in sorted(need, key=lambda s: -need[s]):
@@ -159,11 +164,8 @@ def rank_program(g, core, T, topo):
     def fill(out, v, waw=False):
         run("V", lambda: g.vector.memset(out[0], v), out, [], waw)
 
-    def ac(out, a, func=act.Copy, scale=1.0):
-        if scale == 1.0:
-            run("A", lambda: g.scalar.activation(out[0], a[0], func), out, [a])
-        else:
-            run("A", lambda: g.scalar.activation(out[0], a[0], func, scale=scale), out, [a])
+    def ac(out, a, func=act.Copy, **kw):
+        run("A", lambda: g.scalar.activation(out[0], a[0], func, **kw), out, [a])
 
     def mm(out, l, r, start, stop):
         run("P", lambda: g.tensor.matmul(out[0], l[0], r[0], start, stop), out, [l, r])
@@ -197,22 +199,40 @@ def rank_program(g, core, T, topo):
     arrives("BA1", 0, K, prv)
     arrives("BA2", 0, K, prv2)
 
-    dma("S", b("STK"), (T.stk[:, :], []), "ldSTK")
     dma("S", b("X"), (T.xt[:, :], []), "ldX")
-    dma("A", b("WI"), (T.w[:, :], []), "ldWI")
+    dma("A", b("STK"), (T.stk[:, :], []), "ldSTK")
     dma("A", b("LN8", p1=8), (T.ln[:, :], []), "ldLN8")
+    dma("A", b("WI"), (T.w[:, :], []), "ldWI")
     dma("A", b("Z0", 0, K), (T.z[:, :], []), "ldZ0")
-    dma("A", b("BA0"), (T.bas[:, :], []), "ldBA0")
     dma("A", b("CON"), (T.con[:, :], []), "ldCON")
+    dma("A", b("BA0"), (T.bas[:, :], []), "ldBA0")
 
-    fill(b("ONE"), 1.0)
-    select(b("E", p1=16), b("ONE", p1=16), [[0, 32], [-1, 16]], op.is_equal, 0.0, 0, 1)
+    fill(b("ON16", p1=16), 1.0)
     iota(b("KC", p1=16), [[0, 1]], 0, 1)
-    mm(b("PX", 0, 1), b("E", 0, 128, p1=16), b("KC", p1=16), True, True)
-    cp(b("RC"), b("PX", 0, 1))
+    select(b("E", p1=16), b("ON16", p1=16), [[0, 32], [-1, 16]], op.is_equal, 0.0, 0, 1)
+    mm(b("UU", 0, 1), b("E", 0, 128, p1=16), b("KC", p1=16), True, True)
+    fill(b("ONE"), 1.0)
+    for t in range(3): fill(b("L2S", 64 * t, 64 * t + 64, p1=16), float(TOP + (t + 1) * NP))
+    iota(b("KI"), [[16, 32]], 0, 0)
+    select(b("TA"), b("ONE"), [[-1, 128]], op.is_equal, 0.0, 0, 1)
+    select(b("TB", 0, 9), b("ONE", 0, 9), [[-16, 9]], op.is_ge, 0.0, 0, 1)
+    select(b("TB", 16, 25), b("TB", 0, 9), [[16, 9]], op.is_ge, 0.0, 15, -1)
+    select(b("TC", p1=8), b("ONE", p1=8), [[1, 128]], op.is_ge, 0.0, 0, -16)
+    select(b("TD", p1=8), b("TC", p1=8), [[-1, 128]], op.is_ge, 0.0, 15, 16)
+    for t in range(3):
+        select(b("L2T", 64 * t, 64 * t + 64, p1=16), b("L2S", 64 * t, 64 * t + 64, p1=16), [[1, 64]], op.is_ge, -float(TOP), -1, -1)
+    iota(b("LB", 0, 32), [[16384, 32]], 8192, 0)
+    iota(b("LB", 32, 64), [[16384, 32]], -8192, 0)
+    for n in ("LW0", "LW1"): iota(b(n, 528, 560), [[32, 32]], 0, 0)
+    fill(b("BQ"), 0.0)
+    fill(b("D1A"), -1.0)
+    cp(b("RC"), b("UU", 0, 1))
+    fill(b("D1B"), -1.0)
     ts(b("IC"), b("RC"), 16384.0, op.mult)
     ts(b("SE0"), b("STK"), b("IC"), op.add)
     cp(b("SU0"), b("STK"))
+    cp(b("ID"), b("TA"))
+    fill((T.GE[:, :, 0:256:16], [("GE0", 0, K)]), 1.0)
 
     def rotations(t):
         se = b("SE%d" % t)
@@ -224,27 +244,14 @@ def rank_program(g, core, T, topo):
     yall = [("Y", 0, 1600000)]
     rotations(0)
 
-    select(b("TA"), b("ONE", 0, 128), [[-1, 128]], op.is_equal, 0.0, 0, 1)
-    cp(b("ID"), b("TA"))
     ts(b("ND"), b("TA"), -1.0, op.mult)
-    cp(b("IH"), b("TA"))
-    mm(b("PX"), b("E", 0, 128, p1=16), b("E", p1=16), True, True)
-    cp(b("DG"), b("PX"))
-    select(b("TB", 0, 9), b("ONE", 0, 9), [[-16, 9]], op.is_ge, 0.0, 0, 1)
-    select(b("TB", 16, 25), b("TB", 0, 9), [[16, 9]], op.is_ge, 0.0, 15, -1)
-    fill(b("BQ"), 0.0)
+    ts(b("HI"), b("TA"), 0.5, op.mult)
+    ts(b("KW"), b("KI"), b("RC"), op.add)
     cp(b("BQ", 15, 144, 16), b("TB", 16, 25), True)
     cp(b("WF"), b("WI"))
-    ts(b("BW"), b("BQ"), b("WF"), op.mult)
-    fill(b("MK"), 1.0)
-    fill(b("MK", 0, 2048, 16), 0.0, True)
-    fill((T.GE[:, :, 0:256:16], [("GE", 0, 8192)]), 1.0)
-    iota(b("KI"), [[16, 32]], 0, 0)
-    ts(b("KW"), b("KI"), b("RC"), op.add)
     ts(b("K16"), b("KW"), 16.0, op.mult)
     ts(b("K5"), b("KW"), 512.0, op.add)
-    fill(b("D1A"), -1.0)
-    fill(b("D1B"), -1.0)
+    ts(b("BW"), b("BQ"), b("WF"), op.mult)
     fill(b("D1A", 0, K, 16), 15.0, True)
     for l0, l1 in CHUNKS:
         n, c0, c1 = l1 - l0, l0 // 16, l1 // 16
@@ -252,31 +259,30 @@ def rank_program(g, core, T, topo):
         ts(b("D1A", l0 + 15, l1, 16), b("K16", c0, c1), float(16 * n + 14 - 16 * l0), op.add, waw=True)
         fill(b("D1B", l0, l1, 16), float(16 * n + 14), True)
         ts(b("D1B", l0 + 15, l1, 16), b("K16", c0, c1), float(15 - 16 * l0), op.add, waw=True)
+    fill(b("MK"), 1.0)
+    fill(b("MK", 0, 2048, 16), 0.0, True)
     for t in range(3): fill(b("Z%d" % t, K, 528), 0.0)
-    iota(b("LB", 0, 32), [[16384, 32]], 8192, 0)
-    iota(b("LB", 32, 64), [[16384, 32]], -8192, 0)
+    for n in ("LW0", "LW1"): fill(b(n, 512, 528), 32.0)
+    for n in ("CM0", "CM1"): fill(b(n, 512, 528), -1.0)
     fill(b("LB", 48, 64), -1048576.0, True)
-    for t in range(3): fill(b("L2S", 64 * t, 64 * t + 64, p1=16), float(TOP + (t + 1) * NP))
-    for t in range(3):
-        select(b("L2T", 64 * t, 64 * t + 64, p1=16), b("L2S", 64 * t, 64 * t + 64, p1=16), [[1, 64]], op.is_ge, -float(TOP), -1, -1)
-    mm(b("PX", 0, 192), b("E", 0, 128, p1=16), b("L2T", p1=16), True, True)
-    cp(b("L2"), b("PX", 0, 192))
-    select(b("TA", p1=8), b("ONE", 0, 128, p1=8), [[1, 128]], op.is_ge, 0.0, 0, -16)
-    select(b("TB", p1=8), b("TA", p1=8), [[-1, 128]], op.is_ge, 0.0, 15, 16)
-    cp(b("GA", p1=8), b("TB", p1=8))
+    fill(b("HQ"), -1.0 / 512.0)
+    fill(b("ONB"), 1.0)
+    cp(b("GA", p1=8), b("TD", p1=8))
     cp(b("LNB", p1=8), b("LN8", p1=8))
     mm(b("PX"), b("GA", p1=8), b("LNB", p1=8), True, True)
-    ac(b("LW0", 0, K), b("PX"), scale=512.0)
+    mm(b("VV", 0, 192), b("E", 0, 128, p1=16), b("L2T", p1=16), True, True)
+    ac(b("LW0", 0, K), b("PX"), scale=32.0)
+    cp(b("L2"), b("VV", 0, 192))
     ts(b("LX"), b("PX"), b("RC"), op.is_gt, float(TOP), op.mult)
     tt(b("CM0", 0, K), b("LX"), b("CON"), op.add)
-    for n in ("LW0", "LW1"):
-        fill(b(n, 512, 528), 512.0)
-        iota(b(n, 528, 560), [[512, 32]], 0, 0)
-    for n in ("CM0", "CM1"): fill(b(n, 512, 528), -1.0)
 
     send(b("BA0"), "BA1", 0, K, nxt)
     send(b("BA0"), "BA2", 0, K, nxt2)
 
+    NC = len(CHUNKS)
+    w = lambda n: b("f_" + n)
+    x = lambda n: b("i_" + n)
+    later = []
     for t in range(ROUNDS):
         last = t == ROUNDS - 1
         SU, SE, Z, BA = "SU%d" % t, "SE%d" % t, "Z%d" % t, "BA%d" % t
@@ -289,50 +295,57 @@ def rank_program(g, core, T, topo):
             l0, l1 = CHUNKS[ci]
             ac(b("RP", 32 * l0, 32 * l0 + 16 * (l1 - l0)), ind("X", 0, NREC, SU, l0, l1))
 
+        def ge(l0, l1, i):
+            return (T.GE[:, l0 // 16:l1 // 16, i:256:16], [("GE%d" % i, l0, l1)])
+
+        def row(l0, l1, i):
+            a0, a1 = 32 * l0, 32 * l0 + 16 * (l1 - l0)
+            return (T.RP[:, a0 + i:a1:16], [("RP", a0, a1)])
+
         def compare(ci):
             l0, l1 = CHUNKS[ci]
-            c0, c1, a0, n = l0 // 16, l1 // 16, 32 * l0, 16 * (l1 - l0)
+            a0, n = 32 * l0, 16 * (l1 - l0)
             for i in range(1, 16):
-                tt((T.GE[:, c0:c1, i:256:16], [("GE", 256 * c0, 256 * c1)]), (T.RP[:, a0 + i:a0 + n:16], [("RP", a0, a0 + n)]),
-                   b("ZP", l0, l1), op.is_ge)
+                tt(ge(l0, l1, i), row(l0, l1, i), b("ZP", l0, l1), op.is_ge)
             scan(b("RP", a0 + n, a0 + 2 * n), b("MK", 0, n), b("RP", a0, a0 + n), op.mult, op.max)
 
         def votes(ci):
             l0, l1 = CHUNKS[ci]
-            c0, c1 = l0 // 16, l1 // 16
             for r in range(16):
-                mm(b("VT%d" % (ci % 4), 0, l1 - l0), b("BQ", 15 - r, 143 - r),
-                   (T.GE[:, c0:c1, 16 * r:16 * r + 16], [("GE", 256 * c0, 256 * c1)]), r == 0, r == 15)
+                mm(b("VT%d" % (ci % 2), 0, l1 - l0), b("BQ", 15 - r, 143 - r),
+                   (T.GE[:, l0 // 16:l1 // 16, 16 * r:16 * r + 16], [("GE%d" % i, l0, l1) for i in range(16)]), r == 0, r == 15)
 
         def handler(ci):
             l0, l1 = CHUNKS[ci]
             c0, c1 = l0 // 16, l1 // 16
-            ts(b("T1", l0, l1), b("VT%d" % (ci % 4), 0, l1 - l0), 8.0, op.is_lt, 32768.0, op.mult)
+            ts(b("T1", l0, l1), b("VT%d" % (ci % 2), 0, l1 - l0), 7.5, op.is_lt, 32768.0, op.mult)
             scan(b("OA", l0, l1), b("T1", l0, l1), b("D1A", l0, l1), op.min, op.add)
             scan(b("OB", l0, l1), b("T1", l0, l1), b("D1B", l0, l1), op.min, op.add)
             cp(b("MLu", c0, c1), b("OA", l0 + 15, l1, 16))
             cp(b("ALu", c0, c1), b("OB", l0 + 15, l1, 16))
-            cp(b("M16", l0, l1), ind("RP", 32 * l0, 32 * l1, "MLu", c0, c1))
 
         def taken(ci):
             l0, l1 = CHUNKS[ci]
+            ac(b("MB", l0, l1), ind("RP", 32 * l0, 32 * l1, "MLu", l0 // 16, l1 // 16))
             ac(b("AG", l0, l1), ind("RP", 32 * l0, 32 * l1, "ALu", l0 // 16, l1 // 16))
 
-        for ci in range(3): records(ci)
-        for ci in range(5):
+        records(0)
+        records(1)
+        for ci in range(NC):
             compare(ci)
             votes(ci)
+            if ci + 2 < NC: records(ci + 2)
+            if ci == LATER:
+                for f in later: f()
+                later = []
             if ci:
                 handler(ci - 1)
-                if ci + 2 < 5: records(ci + 2)
                 taken(ci - 1)
-        handler(4)
-        taken(4)
-        for r in range(16): mm(b("UU", 0, 32), b("BW", 15 - r, 143 - r), b("M16", r, K, 16), r == 0, r == 15)
+        handler(NC - 1)
+        taken(NC - 1)
+        for r in range(16): mm(b("UU", 0, 32), b("BW", 15 - r, 143 - r), b("MB", r, K, 16), r == 0, r == 15)
         for r in range(16): mm(b("VV", 0, 32), b("BQ", 15 - r, 143 - r), b("AG", r, K, 16), r == 0, r == 15)
 
-        w = lambda n: b("f_" + n)
-        x = lambda n: b("i_" + n)
         tt(w("h"), b("OA", 15, K, 16), b("KH"), op.subtract)
         ts(w("zq"), w("h"), 16.0, op.is_ge, 512.0, op.mult)
         ts(w("u20"), w("h"), 16.0, op.is_ge, float(NP), op.mult)
@@ -340,6 +353,9 @@ def rank_program(g, core, T, topo):
         ts(w("h5"), w("h"), 512.0, op.mult)
         cp(b("zlu"), w("zl"))
         tt(w("h1k"), w("h5"), b("K5"), op.add)
+        ts(w("h528"), w("h"), 528.0, op.add)
+        cp(b("huu"), w("h"))
+        tt(b(CMc, 528, 1040), ind("L2", 64 * t, 64 * t + 64, "huu"), b(SE), op.add)
         cp(x("ui"), b("UU", 0, 32))
         ts(x("u"), x("ui"), 4095, op.bitwise_and)
         tt(x("u2"), x("u"), x("u"), op.mult)
@@ -348,71 +364,75 @@ def rank_program(g, core, T, topo):
         ts(x("v"), x("vi"), 3, op.bitwise_and)
         if t: ts(w("w0"), x("u"), b("ACOL"), op.add)
         ts(w("np0"), x("v"), 0.0, op.is_equal, float(NP), op.mult)
-        tt(w("np"), w("np0"), w("u20"), op.max)
-        tt(w("w1"), w("w0") if t else x("u"), w("np"), op.add)
-        tt(x("j0"), x("q"), w("w1"), op.add)
         if not last: ts(x("x15"), x("u"), 15, op.bitwise_and)
-        ts(x("j"), x("j0"), NP + 511, op.bitwise_and)
+        tt(w("np"), w("np0"), w("u20"), op.max)
         if not last: tt(x("xk"), x("x15"), b("K16"), op.add)
-        ts(b("jlu"), x("j"), 512.0, op.min)
+        tt(w("w1"), w("w0") if t else x("u"), w("np"), op.add)
         ts(w("n32"), w("np"), 1.0 / 32768.0, op.mult)
-        tt(b("LM"), ind(LWc, 0, 528, "jlu"), b("DG"), op.mult)
-        if not last: cp(b("xlu"), x("xk"))
+        tt(x("j0"), x("q"), w("w1"), op.add)
         tt(w("hl"), w("n32"), w("h"), op.add)
-        scan(b("LS"), b("MK", 0, K), b("LM"), op.mult, op.add)
+        ts(x("j"), x("j0"), NP + 511, op.bitwise_and)
         cp(b("hlu"), w("hl"))
-        tt(x("d"), w("h1k"), b("LS", 15, K, 16), op.subtract)
-        tt(b("BE"), ind("LB", 0, 64, "hlu"), b(BA), op.add)
-        ts(x("dd"), x("d"), 8191, op.bitwise_and)
-        tt(b("PB"), ind(CMc, 0, 528, "jlu"), b("BE"), op.max)
-        cp(b("ylu"), x("dd"))
+        ts(b("jlu"), x("j"), 512.0, op.min)
+        if not last: cp(b("xlu"), x("xk"))
         ac(b("ZZ"), ind(Z, 0, 528, "zlu"))
-        mm(b("VT3"), b("ID"), b("AG"), True, False)
-        mm(b("VT3"), b("ND"), b("ZZ"), False, True)
+        ac(b("LG"), ind(LWc, 0, 528, "jlu"))
+        mm(b("DF0"), b("ID"), b("AG"), True, False)
+        mm(b("DF0"), b("ND"), b("ZZ"), False, True)
+        for r in range(16): mm(b("PX", 0, 32), b("BQ", 15 - r, 143 - r), b("LG", r, K, 16), r == 0, r == 15)
         if not last:
+            mm(b("DF1"), b("HQ"), b("ONB"), True, False)
+            mm(b("DF1"), b("HI"), b("MB"), False, False)
             ac(b("OX"), ind("X", 0, NREC, "xlu"))
-            mm(b("VT2"), b("IH"), b("M16"), True, False)
-            mm(b("VT2"), b("ID"), b("OX"), False, True)
-        ac(b("ZO%d" % t), b("VT3"), act.Abs)
+            mm(b("DF1"), b("HI"), b("OX"), False, True)
+        ac(b("ZO%d" % t), b("DF0"), act.Abs)
+        tt(b("BE"), ind("LB", 0, 64, "hlu"), b(BA), op.add)
+        tt(b("PB"), ind(CMc, 0, 528, "jlu"), b("BE"), op.max)
+
+        def pieces():
+            ts(w("p5"), w("np"), 1.0, op.is_lt, 528.0, op.mult)
+            ts(w("pz"), w("np"), 1.0, op.is_lt)
+            tt(w("cl"), w("p5"), b("KW"), op.add)
+            tt(w("lp"), w("h528"), w("pz"), op.mult)
+            cp(b("clu"), w("cl"))
+            tt(w("ll"), w("lp"), b("KW"), op.max)
+            cp(b("llu"), w("ll"))
+            cf_old = b("CON") if t == 0 else b("CF%d" % ((t + 1) % 2))
+            tt(b("CFI") if last else b("CF%d" % (t % 2)), ind(CMc, 0, 1040, "clu"), cf_old, op.max)
+
+        if last: pieces()
+        tt(x("d"), w("h1k"), b("PX", 0, 32), op.subtract)
+        ts(x("dd"), x("d"), 8191, op.bitwise_and)
+        cp(b("ylu"), x("dd"))
         yi = ind("Y", 0, 16 * K, "ylu")
         tt(b("TY"), (yi[0], yall + yi[1][1:]), b("PB"), op.max)
         ts(b("SN"), b("TY"), 8191, op.bitwise_and)
         if not last:
             cp(b("UO%d" % t), b("SN"))
-            ts(b("EO%d" % t), b("SN"), b("IC"), op.add)
             send(b("ZO%d" % t), "Z%d" % (t + 1), 0, K, nxt)
             send(b("UO%d" % t), "SU%d" % (t + 1), 0, K, nxt)
-            send(b("EO%d" % t), "SE%d" % (t + 1), 0, K, nxt)
-            ts(b("NR"), b("VT2"), 0.5, op.mult, -0.25, op.add)
+            ac(b("NF"), b("DF1"), act.Identity, bias=WHOLE)
+            ac(b("NB"), b("NF"), act.Identity, bias=-WHOLE)
             si = ind("X", 0, NREC, "xlu")
-            cp((si[0], si[1][:1], si[1][1:]), b("NR"))
+            cp((si[0], si[1][:1], si[1][1:]), b("NB"))
+            ts(b("EO%d" % t), b("SN"), b("IC"), op.add)
+            send(b("EO%d" % t), "SE%d" % (t + 1), 0, K, nxt)
+            pieces()
+            later.append(lambda a=LWn, c=LWc: ac(b(a, 0, K), ind(c, 0, 560, "llu")))
+            later.append(lambda a=CMn, c=CMc: ac(b(a, 0, K), ind(c, 0, 1040, "clu")))
+            ts(w("un"), w("h"), 16.0, op.is_ge)
+            run("V", lambda: g.vector.tensor_reduce(T.RED[:, :], w("un")[0], AxisListType.X, op.add), b("RED"), [w("un")])
+            mm(b("VV", 0, 1), b("ONE"), b("RED"), True, True)
+            cp(b("ACOL"), b("VV", 0, 1))
         else:
             cp(b("FO"), b("SN"))
             dma("S", (T.ys[:, :], []), b("FO"), "oS")
             dma("S", (T.yz[:, :], []), b("ZO%d" % t), "oZ")
-        tt(b(CMc, 528, 1040), ind("L2", 64 * t, 64 * t + 64, "hlu"), b(SE), op.add)
-        ts(w("p5"), w("np"), 1.0, op.is_lt, 528.0, op.mult)
-        ts(w("pz"), w("np"), 1.0, op.is_lt)
-        ts(w("h528"), w("h"), 528.0, op.add)
-        tt(w("cl"), w("p5"), b("KW"), op.add)
-        tt(w("lp"), w("h528"), w("pz"), op.mult)
-        cp(b("clu"), w("cl"))
-        tt(w("ll"), w("lp"), b("KW"), op.max)
-        cf_old = b("CON") if t == 0 else b("CF%d" % ((t + 1) % 2))
-        tt(b("CFI") if last else b("CF%d" % (t % 2)), ind(CMc, 0, 1040, "clu"), cf_old, op.max)
-        cp(b("llu"), w("ll"))
-        ac(b(LWn, 0, K), ind(LWc, 0, 560, "llu"))
-        if not last:
-            ac(b(CMn, 0, K), ind(CMc, 0, 1040, "clu"))
-            ts(w("un"), w("h"), 16.0, op.is_ge)
-            run("V", lambda: g.vector.tensor_reduce(T.RED[:, :], w("un")[0], AxisListType.X, op.add), b("RED"), [w("un")])
-            mm(b("PX", 0, 1), b("ONE", 0, 128), b("RED"), True, True)
-            cp(b("ACOL"), b("PX", 0, 1))
-        else:
-            ts(b("TY"), b("CFI"), 8191, op.bitwise_and)
-            cp(b("FC"), b("TY"))
+            ts(b("FI"), b("CFI"), 8191, op.bitwise_and)
+            cp(b("FC"), b("FI"))
             dma("S", (T.yc[:, :], []), b("FC"), "oC")
-            ac(b("FN"), b(LWn, 0, K), scale=1.0 / 512.0)
+            ac(b(LWn, 0, K), ind(LWc, 0, 560, "llu"))
+            ac(b("FN"), b(LWn, 0, K), scale=1.0 / 32.0)
             dma("S", (T.yn[:, :], []), (T.FN[0:128:16, :], [("FN", 0, K)]), "oN")
 
     for s in SEMAPHORES:

@@ -3,6 +3,7 @@ from concourse.mybir import AluOpType, AxisListType, ActivationFunctionType
 ROUNDS, STEP, K, NREC = 3, 3, 512, 8192
 EDGES = [0, 64, 192, 320, 448, 512]
 CHUNKS = list(zip(EDGES[:-1], EDGES[1:]))
+HALVES = [(0, 256), (256, 512)]
 LATER = 2
 NP = 1 << 20
 TOP = 1 << 22
@@ -10,7 +11,8 @@ WHOLE = 12582912.0
 
 SCRATCH = {
     "X": ("sbuf", [128, NREC], "bfloat16"),
-    "RP": ("sbuf", [128, 2 * NREC], "bfloat16"),
+    "RB": ("sbuf", [128, NREC + 32], "bfloat16"),
+    "PM": ("sbuf", [128, NREC], "bfloat16"),
     "GE": ("sbuf", [128, 32, 256], "bfloat16"),
     "Y": ("sbuf", [128, 16 * K], "int32"),
     "D": ("dram", [8, 32, K], "int32"),
@@ -20,14 +22,14 @@ SCRATCH = {
     "CM0": ("sbuf", [128, 1040], "float32"), "CM1": ("sbuf", [128, 1040], "float32"),
     "LW0": ("sbuf", [128, 560], "bfloat16"), "LW1": ("sbuf", [128, 560], "bfloat16"),
     "CF0": ("sbuf", [128, K], "float32"), "CF1": ("sbuf", [128, K], "float32"), "CFI": ("sbuf", [128, K], "int32"),
-    "MB": ("sbuf", [128, K], "bfloat16"), "AG": ("sbuf", [128, K], "bfloat16"), "ZZ": ("sbuf", [128, K], "bfloat16"),
+    "ZM": ("sbuf", [128, 2 * K], "bfloat16"), "AG": ("sbuf", [128, K], "bfloat16"),
     "OX": ("sbuf", [128, K], "bfloat16"), "NF": ("sbuf", [128, K], "float32"), "NB": ("sbuf", [128, K], "bfloat16"),
-    "T1": ("sbuf", [128, K], "bfloat16"), "OA": ("sbuf", [128, K], "float32"), "OB": ("sbuf", [128, K], "float32"),
+    "T1": ("sbuf", [128, K], "bfloat16"), "OA": ("sbuf", [128, K], "float32"),
     "LG": ("sbuf", [128, K], "bfloat16"),
     "BE": ("sbuf", [128, K], "float32"), "PB": ("sbuf", [128, K], "float32"), "TY": ("sbuf", [128, K], "int32"),
     "SN": ("sbuf", [128, K], "int32"), "FO": ("sbuf", [128, K], "float32"), "FC": ("sbuf", [128, K], "float32"),
     "FI": ("sbuf", [128, K], "int32"), "FN": ("sbuf", [128, K], "float32"),
-    "E": ("sbuf", [128, K], "float32"), "ONE": ("sbuf", [128, 128], "float32"), "ON16": ("sbuf", [128, K], "float32"),
+    "E": ("sbuf", [128, 128], "float32"), "ONE": ("sbuf", [128, 128], "float32"),
     "KC": ("sbuf", [128, 1], "float32"),
     "RC": ("sbuf", [128, 1], "float32"), "IC": ("sbuf", [128, 1], "float32"),
     "TA": ("sbuf", [128, 128], "float32"), "TB": ("sbuf", [128, 32], "float32"),
@@ -36,7 +38,7 @@ SCRATCH = {
     "HQ": ("sbuf", [128, 128], "bfloat16"), "ONB": ("sbuf", [128, K], "bfloat16"),
     "BQ": ("sbuf", [128, 144], "bfloat16"), "BW": ("sbuf", [128, 144], "float16"),
     "GA": ("sbuf", [128, 128], "bfloat16"), "MK": ("sbuf", [128, 2048], "bfloat16"),
-    "D1A": ("sbuf", [128, K], "float32"), "D1B": ("sbuf", [128, K], "float32"),
+    "D1A": ("sbuf", [128, K], "float32"),
     "KW": ("sbuf", [128, 32], "float32"), "K16": ("sbuf", [128, 32], "float32"), "KH": ("sbuf", [128, 32], "float32"),
     "K5": ("sbuf", [128, 32], "float32"), "KI": ("sbuf", [128, 32], "float32"),
     "LB": ("sbuf", [128, 64], "float32"), "L2": ("sbuf", [128, 192], "float32"), "L2S": ("sbuf", [128, 192], "float32"),
@@ -49,7 +51,7 @@ for _n in BANKS:
 for _t in range(3):
     SCRATCH["SU%d" % _t] = ("sbuf", [128, K], "uint16")
     SCRATCH["SE%d" % _t] = ("sbuf", [128, K], "int32")
-    SCRATCH["Z%d" % _t] = ("sbuf", [128, 528], "bfloat16")
+    SCRATCH["Z%d" % _t] = ("sbuf", [128, K], "bfloat16")
     SCRATCH["BA%d" % _t] = ("sbuf", [128, K], "int32")
     SCRATCH["ZO%d" % _t] = ("sbuf", [128, K], "bfloat16")
     if _t < 2:
@@ -57,7 +59,7 @@ for _t in range(3):
         SCRATCH["EO%d" % _t] = ("sbuf", [128, K], "int32")
 WF32 = ["h", "un", "u20", "zq", "zl", "h5", "h1k", "np0", "np", "w0", "w1", "n32", "hl", "p5", "cl", "pz", "h528", "lp", "ll"]
 WI32 = ["vi", "v", "ui", "u", "u2", "q", "j0", "j", "d", "dd", "x15", "xk"]
-WU16 = ["MLu", "ALu", "zlu", "jlu", "hlu", "ylu", "xlu", "clu", "llu", "huu"]
+WU16 = ["MLu", "zlu", "jlu", "hlu", "ylu", "xlu", "clu", "llu", "huu"]
 SCRATCH["FW"] = ("sbuf", [128, 32 * len(WF32)], "float32")
 SCRATCH["IW"] = ("sbuf", [128, 32 * len(WI32)], "int32")
 SCRATCH["LU"] = ("sbuf", [128, 32 * len(WU16)], "uint16")
@@ -67,7 +69,7 @@ for _i, _n in enumerate(WI32): TILE["i_" + _n] = ("IW", 32 * _i)
 for _i, _n in enumerate(WU16): TILE[_n] = ("LU", 32 * _i)
 
 LOADS = ["STK", "X", "Z0", "WI", "LN8", "BA0", "CON"]
-ARR = ["SU1", "SU2", "SE1", "SE2", "Z1", "Z2", "BA1", "BA2"]
+ARR = ["SU1a", "SU1b", "SU2a", "SU2b", "SE1", "SE2", "Z1", "Z2", "BA1", "BA2"]
 SEMAPHORES = (["sV", "sA", "sP", "sG", "local", "dD", "dY", "oS", "oZ", "oC", "oN"]
               + ["ld" + n for n in LOADS] + ["ar" + n for n in ARR])
 
@@ -176,42 +178,42 @@ def rank_program(g, core, T, topo):
     def select(out, a, pattern, cmp, fillv, base, cm):
         run("G", lambda: g.affine_select(out[0], a[0], pattern, cmp, fillv, base, cm), out, [a])
 
-    def send(src, dst_name, lo, hi, dst):
+    def send(src, dst_name, lo, hi, dst, part=""):
         await_deps("G", src[1], [], False)
         rid, pid, _se = topo.addr(dst)
         m = topo.mask(core, dst)
         n = len(topo.engines(core, dst))
-        g.remote_dma(T[dst_name][:, lo:hi], src[0], T.sem["ar" + dst_name], T.sem["local"], pid, rid, m)
+        g.remote_dma(T[dst_name][:, lo:hi], src[0], T.sem["ar" + dst_name + part], T.sem["local"], pid, rid, m)
         total["local"] += n
 
-    def arrives(name, lo, hi, src):
+    def arrives(name, lo, hi, src, part=""):
         n = len(topo.engines(src, core))
-        total["ar" + name] += n
-        note("remote", None, [], [(name, lo, hi)], "ar" + name, n)
+        total["ar" + name + part] += n
+        note("remote", None, [], [(name, lo, hi)], "ar" + name + part, n)
 
     nxt = T.cores[(rank + STEP) % len(T.cores)]
     nxt2 = T.cores[(rank + 2 * STEP) % len(T.cores)]
     prv = T.cores[(rank - STEP) % len(T.cores)]
     prv2 = T.cores[(rank - 2 * STEP) % len(T.cores)]
-    for n in ("SU", "SE"):
-        for t in (1, 2): arrives("%s%d" % (n, t), 0, K, prv)
-    for t in (1, 2): arrives("Z%d" % t, 0, K, prv)
+    for t in (1, 2):
+        for part, (l0, l1) in zip("ab", HALVES): arrives("SU%d" % t, l0, l1, prv, part)
+        arrives("SE%d" % t, 0, K, prv)
+        arrives("Z%d" % t, 0, K, prv)
     arrives("BA1", 0, K, prv)
     arrives("BA2", 0, K, prv2)
 
+    dma("S", b("STK"), (T.stk[:, :], []), "ldSTK")
     dma("S", b("X"), (T.xt[:, :], []), "ldX")
-    dma("A", b("STK"), (T.stk[:, :], []), "ldSTK")
     dma("A", b("LN8", p1=8), (T.ln[:, :], []), "ldLN8")
     dma("A", b("WI"), (T.w[:, :], []), "ldWI")
     dma("A", b("Z0", 0, K), (T.z[:, :], []), "ldZ0")
     dma("A", b("CON"), (T.con[:, :], []), "ldCON")
     dma("A", b("BA0"), (T.bas[:, :], []), "ldBA0")
 
-    fill(b("ON16", p1=16), 1.0)
-    iota(b("KC", p1=16), [[0, 1]], 0, 1)
-    select(b("E", p1=16), b("ON16", p1=16), [[0, 32], [-1, 16]], op.is_equal, 0.0, 0, 1)
-    mm(b("UU", 0, 1), b("E", 0, 128, p1=16), b("KC", p1=16), True, True)
     fill(b("ONE"), 1.0)
+    iota(b("KC", p1=16), [[0, 1]], 0, 1)
+    select(b("E", p1=16), b("ONE", p1=16), [[0, 8], [-1, 16]], op.is_equal, 0.0, 0, 1)
+    mm(b("UU", 0, 1), b("E", p1=16), b("KC", p1=16), True, True)
     for t in range(3): fill(b("L2S", 64 * t, 64 * t + 64, p1=16), float(TOP + (t + 1) * NP))
     iota(b("KI"), [[16, 32]], 0, 0)
     select(b("TA"), b("ONE"), [[-1, 128]], op.is_equal, 0.0, 0, 1)
@@ -227,7 +229,7 @@ def rank_program(g, core, T, topo):
     fill(b("BQ"), 0.0)
     fill(b("D1A"), -1.0)
     cp(b("RC"), b("UU", 0, 1))
-    fill(b("D1B"), -1.0)
+    fill(b("RB", 8192, 8224), 0.0)
     ts(b("IC"), b("RC"), 16384.0, op.mult)
     ts(b("SE0"), b("STK"), b("IC"), op.add)
     cp(b("SU0"), b("STK"))
@@ -248,20 +250,15 @@ def rank_program(g, core, T, topo):
     ts(b("HI"), b("TA"), 0.5, op.mult)
     ts(b("KW"), b("KI"), b("RC"), op.add)
     cp(b("BQ", 15, 144, 16), b("TB", 16, 25), True)
-    cp(b("WF"), b("WI"))
     ts(b("K16"), b("KW"), 16.0, op.mult)
     ts(b("K5"), b("KW"), 512.0, op.add)
-    ts(b("BW"), b("BQ"), b("WF"), op.mult)
     fill(b("D1A", 0, K, 16), 15.0, True)
     for l0, l1 in CHUNKS:
-        n, c0, c1 = l1 - l0, l0 // 16, l1 // 16
-        ts(b("KH", c0, c1), b("K16", c0, c1), float(16 * n - 1 - 16 * l0), op.add)
-        ts(b("D1A", l0 + 15, l1, 16), b("K16", c0, c1), float(16 * n + 14 - 16 * l0), op.add, waw=True)
-        fill(b("D1B", l0, l1, 16), float(16 * n + 14), True)
-        ts(b("D1B", l0 + 15, l1, 16), b("K16", c0, c1), float(15 - 16 * l0), op.add, waw=True)
+        c0, c1 = l0 // 16, l1 // 16
+        ts(b("KH", c0, c1), b("K16", c0, c1), float(-1 - 16 * l0), op.add)
+        ts(b("D1A", l0 + 15, l1, 16), b("K16", c0, c1), float(14 - 16 * l0), op.add, waw=True)
     fill(b("MK"), 1.0)
     fill(b("MK", 0, 2048, 16), 0.0, True)
-    for t in range(3): fill(b("Z%d" % t, K, 528), 0.0)
     for n in ("LW0", "LW1"): fill(b(n, 512, 528), 32.0)
     for n in ("CM0", "CM1"): fill(b(n, 512, 528), -1.0)
     fill(b("LB", 48, 64), -1048576.0, True)
@@ -270,11 +267,12 @@ def rank_program(g, core, T, topo):
     cp(b("GA", p1=8), b("TD", p1=8))
     cp(b("LNB", p1=8), b("LN8", p1=8))
     mm(b("PX"), b("GA", p1=8), b("LNB", p1=8), True, True)
-    mm(b("VV", 0, 192), b("E", 0, 128, p1=16), b("L2T", p1=16), True, True)
-    ac(b("LW0", 0, K), b("PX"), scale=32.0)
+    mm(b("VV", 0, 192), b("E", p1=16), b("L2T", p1=16), True, True)
+    mm(b("ZP"), b("ID"), b("Z0", 0, K), True, True)
+    cp(b("WF"), b("WI"))
+    ts(b("BW"), b("BQ"), b("WF"), op.mult)
     cp(b("L2"), b("VV", 0, 192))
     ts(b("LX"), b("PX"), b("RC"), op.is_gt, float(TOP), op.mult)
-    tt(b("CM0", 0, K), b("LX"), b("CON"), op.add)
 
     send(b("BA0"), "BA1", 0, K, nxt)
     send(b("BA0"), "BA2", 0, K, nxt2)
@@ -282,32 +280,32 @@ def rank_program(g, core, T, topo):
     NC = len(CHUNKS)
     w = lambda n: b("f_" + n)
     x = lambda n: b("i_" + n)
-    later = []
+    later = [lambda: ac(b("LW0", 0, K), b("PX"), scale=32.0),
+             lambda: tt(b("CM0", 0, K), b("LX"), b("CON"), op.add)]
     for t in range(ROUNDS):
         last = t == ROUNDS - 1
         SU, SE, Z, BA = "SU%d" % t, "SE%d" % t, "Z%d" % t, "BA%d" % t
         CMc, CMn = "CM%d" % (t % 2), "CM%d" % ((t + 1) % 2)
         LWc, LWn = "LW%d" % (t % 2), "LW%d" % ((t + 1) % 2)
         if t: rotations(t)
-        mm(b("ZP"), b("ID"), b(Z, 0, K), True, True)
+        if t: mm(b("ZP"), b("ID"), b(Z, 0, K), True, True)
 
         def records(ci):
             l0, l1 = CHUNKS[ci]
-            ac(b("RP", 32 * l0, 32 * l0 + 16 * (l1 - l0)), ind("X", 0, NREC, SU, l0, l1))
+            ac(b("RB", 16 * l0 + 15, 16 * l1 + 15), ind("X", 0, NREC, SU, l0, l1))
 
         def ge(l0, l1, i):
             return (T.GE[:, l0 // 16:l1 // 16, i:256:16], [("GE%d" % i, l0, l1)])
 
         def row(l0, l1, i):
-            a0, a1 = 32 * l0, 32 * l0 + 16 * (l1 - l0)
-            return (T.RP[:, a0 + i:a1:16], [("RP", a0, a1)])
+            a0, a1 = 16 * l0 + 15, 16 * l1 + 15
+            return (T.RB[:, a0 + i:a1:16], [("RB", a0, a1)])
 
         def compare(ci):
             l0, l1 = CHUNKS[ci]
-            a0, n = 32 * l0, 16 * (l1 - l0)
             for i in range(1, 16):
                 tt(ge(l0, l1, i), row(l0, l1, i), b("ZP", l0, l1), op.is_ge)
-            scan(b("RP", a0 + n, a0 + 2 * n), b("MK", 0, n), b("RP", a0, a0 + n), op.mult, op.max)
+            scan(b("PM", 16 * l0, 16 * l1), b("MK", 0, 16 * (l1 - l0)), b("RB", 16 * l0 + 15, 16 * l1 + 15), op.mult, op.max)
 
         def votes(ci):
             l0, l1 = CHUNKS[ci]
@@ -320,21 +318,26 @@ def rank_program(g, core, T, topo):
             c0, c1 = l0 // 16, l1 // 16
             ts(b("T1", l0, l1), b("VT%d" % (ci % 2), 0, l1 - l0), 7.5, op.is_lt, 32768.0, op.mult)
             scan(b("OA", l0, l1), b("T1", l0, l1), b("D1A", l0, l1), op.min, op.add)
-            scan(b("OB", l0, l1), b("T1", l0, l1), b("D1B", l0, l1), op.min, op.add)
             cp(b("MLu", c0, c1), b("OA", l0 + 15, l1, 16))
-            cp(b("ALu", c0, c1), b("OB", l0 + 15, l1, 16))
 
         def taken(ci):
             l0, l1 = CHUNKS[ci]
-            ac(b("MB", l0, l1), ind("RP", 32 * l0, 32 * l1, "MLu", l0 // 16, l1 // 16))
-            ac(b("AG", l0, l1), ind("RP", 32 * l0, 32 * l1, "ALu", l0 // 16, l1 // 16))
+            ac(b("ZM", K + l0, K + l1), ind("PM", 16 * l0, 16 * l1, "MLu", l0 // 16, l1 // 16))
+            ac(b("AG", l0, l1), ind("RB", 16 * l0 + 16, 16 * l1 + 16, "MLu", l0 // 16, l1 // 16))
+
+        def changes(ci):
+            l0, l1 = CHUNKS[ci]
+            mm(b("DF0", l0, l1), b("ID"), b("AG", l0, l1), True, False)
+            mm(b("DF0", l0, l1), b("ND"), b(Z, l0, l1), False, True)
 
         records(0)
         records(1)
         for ci in range(NC):
             compare(ci)
             votes(ci)
+            if ci >= 2: changes(ci - 2)
             if ci + 2 < NC: records(ci + 2)
+            if ci == 0 and t: cp(b("ACOL"), b("VV", 0, 1))
             if ci == LATER:
                 for f in later: f()
                 later = []
@@ -343,13 +346,15 @@ def rank_program(g, core, T, topo):
                 taken(ci - 1)
         handler(NC - 1)
         taken(NC - 1)
-        for r in range(16): mm(b("UU", 0, 32), b("BW", 15 - r, 143 - r), b("MB", r, K, 16), r == 0, r == 15)
+        for r in range(16): mm(b("UU", 0, 32), b("BW", 15 - r, 143 - r), b("ZM", K + r, 2 * K, 16), r == 0, r == 15)
+        changes(NC - 2)
+        changes(NC - 1)
         for r in range(16): mm(b("VV", 0, 32), b("BQ", 15 - r, 143 - r), b("AG", r, K, 16), r == 0, r == 15)
 
         tt(w("h"), b("OA", 15, K, 16), b("KH"), op.subtract)
         ts(w("zq"), w("h"), 16.0, op.is_ge, 512.0, op.mult)
         ts(w("u20"), w("h"), 16.0, op.is_ge, float(NP), op.mult)
-        tt(w("zl"), w("zq"), b("KW"), op.max)
+        tt(w("zl"), w("zq"), b("KW"), op.add)
         ts(w("h5"), w("h"), 512.0, op.mult)
         cp(b("zlu"), w("zl"))
         tt(w("h1k"), w("h5"), b("K5"), op.add)
@@ -375,17 +380,16 @@ def rank_program(g, core, T, topo):
         cp(b("hlu"), w("hl"))
         ts(b("jlu"), x("j"), 512.0, op.min)
         if not last: cp(b("xlu"), x("xk"))
-        ac(b("ZZ"), ind(Z, 0, 528, "zlu"))
+        ac(b("ZM", 0, K), b("DF0"), act.Abs)
+        ac(b("ZO%d" % t), ind("ZM", 0, 2 * K, "zlu"))
         ac(b("LG"), ind(LWc, 0, 528, "jlu"))
-        mm(b("DF0"), b("ID"), b("AG"), True, False)
-        mm(b("DF0"), b("ND"), b("ZZ"), False, True)
-        for r in range(16): mm(b("PX", 0, 32), b("BQ", 15 - r, 143 - r), b("LG", r, K, 16), r == 0, r == 15)
         if not last:
             mm(b("DF1"), b("HQ"), b("ONB"), True, False)
-            mm(b("DF1"), b("HI"), b("MB"), False, False)
+            mm(b("DF1"), b("HI"), b("ZM", K, 2 * K), False, False)
+        for r in range(16): mm(b("PX", 0, 32), b("BQ", 15 - r, 143 - r), b("LG", r, K, 16), r == 0, r == 15)
+        if not last:
             ac(b("OX"), ind("X", 0, NREC, "xlu"))
             mm(b("DF1"), b("HI"), b("OX"), False, True)
-        ac(b("ZO%d" % t), b("DF0"), act.Abs)
         tt(b("BE"), ind("LB", 0, 64, "hlu"), b(BA), op.add)
         tt(b("PB"), ind(CMc, 0, 528, "jlu"), b("BE"), op.max)
 
@@ -404,17 +408,21 @@ def rank_program(g, core, T, topo):
         tt(x("d"), w("h1k"), b("PX", 0, 32), op.subtract)
         ts(x("dd"), x("d"), 8191, op.bitwise_and)
         cp(b("ylu"), x("dd"))
-        yi = ind("Y", 0, 16 * K, "ylu")
-        tt(b("TY"), (yi[0], yall + yi[1][1:]), b("PB"), op.max)
-        ts(b("SN"), b("TY"), 8191, op.bitwise_and)
+        if not last: send(b("ZO%d" % t), "Z%d" % (t + 1), 0, K, nxt)
         if not last:
-            cp(b("UO%d" % t), b("SN"))
-            send(b("ZO%d" % t), "Z%d" % (t + 1), 0, K, nxt)
-            send(b("UO%d" % t), "SU%d" % (t + 1), 0, K, nxt)
             ac(b("NF"), b("DF1"), act.Identity, bias=WHOLE)
             ac(b("NB"), b("NF"), act.Identity, bias=-WHOLE)
-            si = ind("X", 0, NREC, "xlu")
-            cp((si[0], si[1][:1], si[1][1:]), b("NB"))
+        for half, (l0, l1) in enumerate(HALVES):
+            yi = ind("Y", 0, 16 * K, "ylu", l0 // 16, l1 // 16)
+            tt(b("TY", l0, l1), (yi[0], yall + yi[1][1:]), b("PB", l0, l1), op.max)
+            ts(b("SN", l0, l1), b("TY", l0, l1), 8191, op.bitwise_and)
+            if not last:
+                cp(b("UO%d" % t, l0, l1), b("SN", l0, l1))
+                send(b("UO%d" % t, l0, l1), "SU%d" % (t + 1), l0, l1, nxt, "ab"[half])
+                if half == 0:
+                    si = ind("X", 0, NREC, "xlu")
+                    cp((si[0], si[1][:1], si[1][1:]), b("NB"))
+        if not last:
             ts(b("EO%d" % t), b("SN"), b("IC"), op.add)
             send(b("EO%d" % t), "SE%d" % (t + 1), 0, K, nxt)
             pieces()
@@ -423,7 +431,6 @@ def rank_program(g, core, T, topo):
             ts(w("un"), w("h"), 16.0, op.is_ge)
             run("V", lambda: g.vector.tensor_reduce(T.RED[:, :], w("un")[0], AxisListType.X, op.add), b("RED"), [w("un")])
             mm(b("VV", 0, 1), b("ONE"), b("RED"), True, True)
-            cp(b("ACOL"), b("VV", 0, 1))
         else:
             cp(b("FO"), b("SN"))
             dma("S", (T.ys[:, :], []), b("FO"), "oS")

from concourse.mybir import AluOpType, AxisListType, ActivationFunctionType

ROUNDS, STEP, K, NREC = 3, 3, 512, 8192
EDGES = [0, 64, 192, 320, 448, 512]
CHUNKS = list(zip(EDGES[:-1], EDGES[1:]))
HALVES = [(0, 256), (256, 512)]
LATER = 2
NP = 1 << 20
TOP = 1 << 22
WHOLE = 12582912.0

SCRATCH = {
    "X": ("sbuf", [128, NREC], "bfloat16"),
    "RB": ("sbuf", [128, NREC + 32], "bfloat16"),
    "PM": ("sbuf", [128, NREC], "bfloat16"),
    "GE": ("sbuf", [128, 32, 256], "bfloat16"),
    "Y": ("sbuf", [128, 16 * K], "int32"),
    "D": ("dram", [8, 32, K], "int32"),
    "STK": ("sbuf", [128, K], "int32"), "CON": ("sbuf", [128, K], "int32"),
    "LN8": ("sbuf", [128, K], "int32"), "LNB": ("sbuf", [128, K], "bfloat16"), "LX": ("sbuf", [128, K], "float32"),
    "WI": ("sbuf", [128, 1], "int32"), "WF": ("sbuf", [128, 1], "float32"),
    "CM0": ("sbuf", [128, 1040], "float32"), "CM1": ("sbuf", [128, 1040], "float32"),
    "LW0": ("sbuf", [128, 560], "bfloat16"), "LW1": ("sbuf", [128, 560], "bfloat16"),
    "CF0": ("sbuf", [128, K], "float32"), "CF1": ("sbuf", [128, K], "float32"), "CFI": ("sbuf", [128, K], "int32"),
    "ZM": ("sbuf", [128, 2 * K], "bfloat16"), "AG": ("sbuf", [128, K], "bfloat16"),
    "OX": ("sbuf", [128, K], "bfloat16"), "NF": ("sbuf", [128, K], "float32"), "NB": ("sbuf", [128, K], "bfloat16"),
    "T1": ("sbuf", [128, K], "bfloat16"), "OA": ("sbuf", [128, K], "float32"),
    "LG": ("sbuf", [128, K], "bfloat16"),
    "BE": ("sbuf", [128, K], "float32"), "PB": ("sbuf", [128, K], "float32"), "TY": ("sbuf", [128, K], "int32"),
    "SN": ("sbuf", [128, K], "int32"), "FO": ("sbuf", [128, K], "float32"), "FC": ("sbuf", [128, K], "float32"),
    "FI": ("sbuf", [128, K], "int32"), "FN": ("sbuf", [128, K], "float32"),
    "E": ("sbuf", [128, 128], "float32"), "ONE": ("sbuf", [128, 128], "float32"),
    "KC": ("sbuf", [128, 1], "float32"),
    "RC": ("sbuf", [128, 1], "float32"), "IC": ("sbuf", [128, 1], "float32"),
    "TA": ("sbuf", [128, 128], "float32"), "TB": ("sbuf", [128, 32], "float32"),
    "TC": ("sbuf", [128, 128], "float32"), "TD": ("sbuf", [128, 128], "float32"),
    "ID": ("sbuf", [128, 128], "bfloat16"), "ND": ("sbuf", [128, 128], "bfloat16"), "HI": ("sbuf", [128, 128], "bfloat16"),
    "HQ": ("sbuf", [128, 128], "bfloat16"), "ONB": ("sbuf", [128, K], "bfloat16"),
    "BQ": ("sbuf", [128, 144], "bfloat16"), "BW": ("sbuf", [128, 144], "float16"),
    "GA": ("sbuf", [128, 128], "bfloat16"), "MK": ("sbuf", [128, 2048], "bfloat16"),
    "D1A": ("sbuf", [128, K], "float32"),
    "KW": ("sbuf", [128, 32], "float32"), "K16": ("sbuf", [128, 32], "float32"), "KH": ("sbuf", [128, 32], "float32"),
    "K5": ("sbuf", [128, 32], "float32"), "KI": ("sbuf", [128, 32], "float32"),
    "LB": ("sbuf", [128, 64], "float32"), "L2": ("sbuf", [128, 192], "float32"), "L2S": ("sbuf", [128, 192], "float32"),
    "L2T": ("sbuf", [128, 192], "float32"),
    "ACOL": ("sbuf", [128, 1], "float32"), "RED": ("sbuf", [128, 1], "float32"),
}
BANKS = ["ZP", "UU", "VV", "PX", "VT0", "VT1", "DF0", "DF1"]
for _n in BANKS:
    SCRATCH[_n] = ("psum", [128, K], "float32")
for _t in range(3):
    SCRATCH["SU%d" % _t] = ("sbuf", [128, K], "uint16")
    SCRATCH["SE%d" % _t] = ("sbuf", [128, K], "int32")
    SCRATCH["Z%d" % _t] = ("sbuf", [128, K], "bfloat16")
    SCRATCH["BA%d" % _t] = ("sbuf", [128, K], "int32")
    SCRATCH["ZO%d" % _t] = ("sbuf", [128, K], "bfloat16")
    if _t < 2:
        SCRATCH["UO%d" % _t] = ("sbuf", [128, K], "uint16")
        SCRATCH["EO%d" % _t] = ("sbuf", [128, K], "int32")
WF32 = ["h", "un", "u20", "zq", "zl", "h5", "h1k", "np0", "np", "w0", "w1", "n32", "hl", "p5", "cl", "pz", "h528", "lp", "ll"]
WI32 = ["vi", "v", "ui", "u", "u2", "q", "j0", "j", "d", "dd", "x15", "xk"]
WU16 = ["MLu", "zlu", "jlu", "hlu", "ylu", "xlu", "clu", "llu", "huu"]
SCRATCH["FW"] = ("sbuf", [128, 32 * len(WF32)], "float32")
SCRATCH["IW"] = ("sbuf", [128, 32 * len(WI32)], "int32")
SCRATCH["LU"] = ("sbuf", [128, 32 * len(WU16)], "uint16")
TILE = {}
for _i, _n in enumerate(WF32): TILE["f_" + _n] = ("FW", 32 * _i)
for _i, _n in enumerate(WI32): TILE["i_" + _n] = ("IW", 32 * _i)
for _i, _n in enumerate(WU16): TILE[_n] = ("LU", 32 * _i)

LOADS = ["STK", "X", "Z0", "WI", "LN8", "BA0", "CON"]
ARR = ["SU1a", "SU1b", "SU2a", "SU2b", "SE1", "SE2", "Z1", "Z2", "BA1", "BA2"]
SEMAPHORES = (["sV", "sA", "sP", "sG", "local", "dD", "dY", "oS", "oZ", "oC", "oN"]
              + ["ld" + n for n in LOADS] + ["ar" + n for n in ARR])


def rank_program(g, core, T, topo):
    rank = T.rank_of(core)
    if rank is None:
        return
    op = AluOpType
    act = ActivationFunctionType
    queue = {"V": g.vector, "A": g.scalar, "P": g.tensor, "G": g, "S": g.sync}
    total = {s: 0 for s in SEMAPHORES}
    seen = {q: {} for q in queue}
    snap = {}
    hist = {}

    def learn(q, sem, cnt):
        if seen[q].get(sem, 0) < cnt: seen[q][sem] = cnt
        for s, n in snap.get((sem, cnt), {}).items():
            if seen[q].get(s, 0) < n: seen[q][s] = n

    def await_deps(q, reads, writes, own_waw):
        need = {}
        for lst, isw in ((reads, False), (writes, True)):
            for name, lo, hi in lst:
                ps = name in BANKS
                for l, h, w, oq, sem, cnt in hist.get(name, []):
                    if not ps and (h <= lo or hi <= l): continue
                    if oq == q:
                        if not (w and (not isw or own_waw)): continue
                    elif not (isw or w or ps): continue
                    if seen[q].get(sem, 0) >= cnt: continue
                    if sem[0] in "ldo": cnt = total[sem]
                    if need.get(sem, 0) < cnt: need[sem] = cnt
        for sem in sorted(need, key=lambda s: -need[s]):
            if seen[q].get(sem, 0) < need[sem]:
                queue[q].wait_ge(T.sem[sem], need[sem])
                learn(q, sem, need[sem])

    def note(oq, q, reads, writes, sem, cnt):
        snap[(sem, cnt)] = dict(seen[q]) if q else {}
        for name, lo, hi in writes:
            old = [e for e in hist.get(name, []) if not (lo <= e[0] and e[1] <= hi)]
            hist[name] = old + [(lo, hi, True, oq, sem, cnt)]
        for name, lo, hi in reads:
            old = [e for e in hist.get(name, []) if not (not e[2] and e[3] == oq and lo <= e[0] and e[1] <= hi)]
            hist[name] = old + [(lo, hi, False, oq, sem, cnt)]

    def run(q, fn, out, ins, own_waw=False):
        reads = [x for i in ins for x in i[1]]
        writes = list(out[1])
        for x in out[2:]: reads += x
        await_deps(q, reads, writes, own_waw)
        sem = "s" + q
        total[sem] += 1
        fn().then_inc(T.sem[sem], 1)
        note(q, q, reads, writes, sem, total[sem])

    def dma(q, out, in_, sem, last=True):
        await_deps(q, in_[1], out[1], True)
        total[sem] += 16
        queue[q].dma_start(out[0], in_[0]).then_inc(T.sem[sem], 16)
        note("dma" + sem, q, in_[1], out[1], sem, total[sem])

    def b(name, lo=0, hi=None, step=1, p0=0, p1=128):
        if name in TILE:
            name, o = TILE[name]
            lo, hi = o + lo, o + (32 if hi is None else hi)
        hi = SCRATCH[name][1][-1] if hi is None else hi
        ap = T[name][p0:p1, lo:hi] if step == 1 else T[name][p0:p1, lo:hi:step]
        return (ap, [(name, lo, hi)])

    def ind(name, lo, hi, lst, c0=0, c1=32):
        lst, o = TILE.get(lst, (lst, 0))
        return (T[name][:, lo:hi].indirect(T[lst][:, o + c0:o + c1]), [(name, lo, hi), (lst, o + c0, o + c1)])

    def tt(out, a, c, o):
        run("V", lambda: g.vector.tensor_tensor(out[0], a[0], c[0], o), out, [a, c])

    def ts(out, a, s1, o1, s2=None, o2=None, waw=False):
        ins = [a] + ([s1] if isinstance(s1, tuple) else [])
        v1 = s1[0] if isinstance(s1, tuple) else s1
        if o2 is None:
            run("V", lambda: g.vector.tensor_scalar(out[0], a[0], v1, None, o1), out, ins, waw)
        else:
            run("V", lambda: g.vector.tensor_scalar(out[0], a[0], v1, s2, o1, o2), out, ins, waw)

    def cp(out, a, waw=False):
        run("V", lambda: g.vector.tensor_copy(out[0], a[0]), out, [a], waw)

    def scan(out, a, c, o1, o2):
        run("V", lambda: g.vector.tensor_tensor_scan(out[0], a[0], c[0], 0.0, o1, o2), out, [a, c])

    def fill(out, v, waw=False):
        run("V", lambda: g.vector.memset(out[0], v), out, [], waw)

    def ac(out, a, func=act.Copy, **kw):
        run("A", lambda: g.scalar.activation(out[0], a[0], func, **kw), out, [a])

    def mm(out, l, r, start, stop):
        run("P", lambda: g.tensor.matmul(out[0], l[0], r[0], start, stop), out, [l, r])

    def iota(out, pattern, base, cm):
        run("G", lambda: g.iota(out[0], pattern, base, cm, allow_small_or_imprecise_dtypes=True), out, [])

    def select(out, a, pattern, cmp, fillv, base, cm):
        run("G", lambda: g.affine_select(out[0], a[0], pattern, cmp, fillv, base, cm), out, [a])

    def send(src, dst_name, lo, hi, dst, part=""):
        await_deps("G", src[1], [], False)
        rid, pid, _se = topo.addr(dst)
        m = topo.mask(core, dst)
        n = len(topo.engines(core, dst))
        g.remote_dma(T[dst_name][:, lo:hi], src[0], T.sem["ar" + dst_name + part], T.sem["local"], pid, rid, m)
        total["local"] += n

    def arrives(name, lo, hi, src, part=""):
        n = len(topo.engines(src, core))
        total["ar" + name + part] += n
        note("remote", None, [], [(name, lo, hi)], "ar" + name + part, n)

    nxt = T.cores[(rank + STEP) % len(T.cores)]
    nxt2 = T.cores[(rank + 2 * STEP) % len(T.cores)]
    prv = T.cores[(rank - STEP) % len(T.cores)]
    prv2 = T.cores[(rank - 2 * STEP) % len(T.cores)]
    for t in (1, 2):
        for part, (l0, l1) in zip("ab", HALVES): arrives("SU%d" % t, l0, l1, prv, part)
        arrives("SE%d" % t, 0, K, prv)
        arrives("Z%d" % t, 0, K, prv)
    arrives("BA1", 0, K, prv)
    arrives("BA2", 0, K, prv2)

    dma("S", b("STK"), (T.stk[:, :], []), "ldSTK")
    dma("S", b("X"), (T.xt[:, :], []), "ldX")
    dma("A", b("LN8", p1=8), (T.ln[:, :], []), "ldLN8")
    dma("A", b("WI"), (T.w[:, :], []), "ldWI")
    dma("A", b("Z0", 0, K), (T.z[:, :], []), "ldZ0")
    dma("A", b("CON"), (T.con[:, :], []), "ldCON")
    dma("A", b("BA0"), (T.bas[:, :], []), "ldBA0")

    fill(b("ONE"), 1.0)
    iota(b("KC", p1=16), [[0, 1]], 0, 1)
    select(b("E", p1=16), b("ONE", p1=16), [[0, 8], [-1, 16]], op.is_equal, 0.0, 0, 1)
    mm(b("UU", 0, 1), b("E", p1=16), b("KC", p1=16), True, True)
    for t in range(3): fill(b("L2S", 64 * t, 64 * t + 64, p1=16), float(TOP + (t + 1) * NP))
    iota(b("KI"), [[16, 32]], 0, 0)
    select(b("TA"), b("ONE"), [[-1, 128]], op.is_equal, 0.0, 0, 1)
    select(b("TB", 0, 9), b("ONE", 0, 9), [[-16, 9]], op.is_ge, 0.0, 0, 1)
    select(b("TB", 16, 25), b("TB", 0, 9), [[16, 9]], op.is_ge, 0.0, 15, -1)
    select(b("TC", p1=8), b("ONE", p1=8), [[1, 128]], op.is_ge, 0.0, 0, -16)
    select(b("TD", p1=8), b("TC", p1=8), [[-1, 128]], op.is_ge, 0.0, 15, 16)
    for t in range(3):
        select(b("L2T", 64 * t, 64 * t + 64, p1=16), b("L2S", 64 * t, 64 * t + 64, p1=16), [[1, 64]], op.is_ge, -float(TOP), -1, -1)
    iota(b("LB", 0, 32), [[16384, 32]], 8192, 0)
    iota(b("LB", 32, 64), [[16384, 32]], -8192, 0)
    for n in ("LW0", "LW1"): iota(b(n, 528, 560), [[32, 32]], 0, 0)
    fill(b("BQ"), 0.0)
    fill(b("D1A"), -1.0)
    cp(b("RC"), b("UU", 0, 1))
    fill(b("RB", 8192, 8224), 0.0)
    ts(b("IC"), b("RC"), 16384.0, op.mult)
    ts(b("SE0"), b("STK"), b("IC"), op.add)
    cp(b("SU0"), b("STK"))
    cp(b("ID"), b("TA"))
    fill((T.GE[:, :, 0:256:16], [("GE0", 0, K)]), 1.0)

    def rotations(t):
        se = b("SE%d" % t)
        for half in (0, 1):
            dma("S", (T.D[:, 16 * half:16 * half + 16, :], [("D", 16 * half, 16 * half + 16)]), se, "dD")
        for q in range(16):
            dma("S", (T.Y[q::16, :], [("Y", q * 100000, q * 100000 + 1)]), (T.D[:, q:q + 16, :], [("D", q, q + 16)]), "dY")

    yall = [("Y", 0, 1600000)]
    rotations(0)

    ts(b("ND"), b("TA"), -1.0, op.mult)
    ts(b("HI"), b("TA"), 0.5, op.mult)
    ts(b("KW"), b("KI"), b("RC"), op.add)
    cp(b("BQ", 15, 144, 16), b("TB", 16, 25), True)
    ts(b("K16"), b("KW"), 16.0, op.mult)
    ts(b("K5"), b("KW"), 512.0, op.add)
    fill(b("D1A", 0, K, 16), 15.0, True)
    for l0, l1 in CHUNKS:
        c0, c1 = l0 // 16, l1 // 16
        ts(b("KH", c0, c1), b("K16", c0, c1), float(-1 - 16 * l0), op.add)
        ts(b("D1A", l0 + 15, l1, 16), b("K16", c0, c1), float(14 - 16 * l0), op.add, waw=True)
    fill(b("MK"), 1.0)
    fill(b("MK", 0, 2048, 16), 0.0, True)
    for n in ("LW0", "LW1"): fill(b(n, 512, 528), 32.0)
    for n in ("CM0", "CM1"): fill(b(n, 512, 528), -1.0)
    fill(b("LB", 48, 64), -1048576.0, True)
    fill(b("HQ"), -1.0 / 512.0)
    fill(b("ONB"), 1.0)
    cp(b("GA", p1=8), b("TD", p1=8))
    cp(b("LNB", p1=8), b("LN8", p1=8))
    mm(b("PX"), b("GA", p1=8), b("LNB", p1=8), True, True)
    mm(b("VV", 0, 192), b("E", p1=16), b("L2T", p1=16), True, True)
    mm(b("ZP"), b("ID"), b("Z0", 0, K), True, True)
    cp(b("WF"), b("WI"))
    ts(b("BW"), b("BQ"), b("WF"), op.mult)
    cp(b("L2"), b("VV", 0, 192))
    ts(b("LX"), b("PX"), b("RC"), op.is_gt, float(TOP), op.mult)

    send(b("BA0"), "BA1", 0, K, nxt)
    send(b("BA0"), "BA2", 0, K, nxt2)

    NC = len(CHUNKS)
    w = lambda n: b("f_" + n)
    x = lambda n: b("i_" + n)
    later = [lambda: ac(b("LW0", 0, K), b("PX"), scale=32.0),
             lambda: tt(b("CM0", 0, K), b("LX"), b("CON"), op.add)]
    for t in range(ROUNDS):
        last = t == ROUNDS - 1
        SU, SE, Z, BA = "SU%d" % t, "SE%d" % t, "Z%d" % t, "BA%d" % t
        CMc, CMn = "CM%d" % (t % 2), "CM%d" % ((t + 1) % 2)
        LWc, LWn = "LW%d" % (t % 2), "LW%d" % ((t + 1) % 2)
        if t: rotations(t)
        if t: mm(b("ZP"), b("ID"), b(Z, 0, K), True, True)

        def records(ci):
            l0, l1 = CHUNKS[ci]
            ac(b("RB", 16 * l0 + 15, 16 * l1 + 15), ind("X", 0, NREC, SU, l0, l1))

        def ge(l0, l1, i):
            return (T.GE[:, l0 // 16:l1 // 16, i:256:16], [("GE%d" % i, l0, l1)])

        def row(l0, l1, i):
            a0, a1 = 16 * l0 + 15, 16 * l1 + 15
            return (T.RB[:, a0 + i:a1:16], [("RB", a0, a1)])

        def compare(ci):
            l0, l1 = CHUNKS[ci]
            for i in range(1, 16):
                tt(ge(l0, l1, i), row(l0, l1, i), b("ZP", l0, l1), op.is_ge)
            scan(b("PM", 16 * l0, 16 * l1), b("MK", 0, 16 * (l1 - l0)), b("RB", 16 * l0 + 15, 16 * l1 + 15), op.mult, op.max)

        def votes(ci):
            l0, l1 = CHUNKS[ci]
            for r in range(16):
                mm(b("VT%d" % (ci % 2), 0, l1 - l0), b("BQ", 15 - r, 143 - r),
                   (T.GE[:, l0 // 16:l1 // 16, 16 * r:16 * r + 16], [("GE%d" % i, l0, l1) for i in range(16)]), r == 0, r == 15)

        def handler(ci):
            l0, l1 = CHUNKS[ci]
            c0, c1 = l0 // 16, l1 // 16
            ts(b("T1", l0, l1), b("VT%d" % (ci % 2), 0, l1 - l0), 7.5, op.is_lt, 32768.0, op.mult)
            scan(b("OA", l0, l1), b("T1", l0, l1), b("D1A", l0, l1), op.min, op.add)
            cp(b("MLu", c0, c1), b("OA", l0 + 15, l1, 16))

        def taken(ci):
            l0, l1 = CHUNKS[ci]
            ac(b("ZM", K + l0, K + l1), ind("PM", 16 * l0, 16 * l1, "MLu", l0 // 16, l1 // 16))
            ac(b("AG", l0, l1), ind("RB", 16 * l0 + 16, 16 * l1 + 16, "MLu", l0 // 16, l1 // 16))

        def changes(ci):
            l0, l1 = CHUNKS[ci]
            mm(b("DF0", l0, l1), b("ID"), b("AG", l0, l1), True, False)
            mm(b("DF0", l0, l1), b("ND"), b(Z, l0, l1), False, True)

        records(0)
        records(1)
        for ci in range(NC):
            compare(ci)
            votes(ci)
            if ci >= 2: changes(ci - 2)
            if ci + 2 < NC: records(ci + 2)
            if ci == 0 and t: cp(b("ACOL"), b("VV", 0, 1))
            if ci == LATER:
                for f in later: f()
                later = []
            if ci:
                handler(ci - 1)
                taken(ci - 1)
        handler(NC - 1)
        taken(NC - 1)
        for r in range(16): mm(b("UU", 0, 32), b("BW", 15 - r, 143 - r), b("ZM", K + r, 2 * K, 16), r == 0, r == 15)
        changes(NC - 2)
        changes(NC - 1)
        for r in range(16): mm(b("VV", 0, 32), b("BQ", 15 - r, 143 - r), b("AG", r, K, 16), r == 0, r == 15)

        tt(w("h"), b("OA", 15, K, 16), b("KH"), op.subtract)
        ts(w("zq"), w("h"), 16.0, op.is_ge, 512.0, op.mult)
        ts(w("u20"), w("h"), 16.0, op.is_ge, float(NP), op.mult)
        tt(w("zl"), w("zq"), b("KW"), op.add)
        ts(w("h5"), w("h"), 512.0, op.mult)
        cp(b("zlu"), w("zl"))
        tt(w("h1k"), w("h5"), b("K5"), op.add)
        ts(w("h528"), w("h"), 528.0, op.add)
        cp(b("huu"), w("h"))
        tt(b(CMc, 528, 1040), ind("L2", 64 * t, 64 * t + 64, "huu"), b(SE), op.add)
        cp(x("ui"), b("UU", 0, 32))
        ts(x("u"), x("ui"), 4095, op.bitwise_and)
        tt(x("u2"), x("u"), x("u"), op.mult)
        cp(x("vi"), b("VV", 0, 32))
        ts(x("q"), x("u2"), 5, op.arith_shift_right)
        ts(x("v"), x("vi"), 3, op.bitwise_and)
        if t: ts(w("w0"), x("u"), b("ACOL"), op.add)
        ts(w("np0"), x("v"), 0.0, op.is_equal, float(NP), op.mult)
        if not last: ts(x("x15"), x("u"), 15, op.bitwise_and)
        tt(w("np"), w("np0"), w("u20"), op.max)
        if not last: tt(x("xk"), x("x15"), b("K16"), op.add)
        tt(w("w1"), w("w0") if t else x("u"), w("np"), op.add)
        ts(w("n32"), w("np"), 1.0 / 32768.0, op.mult)
        tt(x("j0"), x("q"), w("w1"), op.add)
        tt(w("hl"), w("n32"), w("h"), op.add)
        ts(x("j"), x("j0"), NP + 511, op.bitwise_and)
        cp(b("hlu"), w("hl"))
        ts(b("jlu"), x("j"), 512.0, op.min)
        if not last: cp(b("xlu"), x("xk"))
        ac(b("ZM", 0, K), b("DF0"), act.Abs)
        ac(b("ZO%d" % t), ind("ZM", 0, 2 * K, "zlu"))
        ac(b("LG"), ind(LWc, 0, 528, "jlu"))
        if not last:
            mm(b("DF1"), b("HQ"), b("ONB"), True, False)
            mm(b("DF1"), b("HI"), b("ZM", K, 2 * K), False, False)
        for r in range(16): mm(b("PX", 0, 32), b("BQ", 15 - r, 143 - r), b("LG", r, K, 16), r == 0, r == 15)
        if not last:
            ac(b("OX"), ind("X", 0, NREC, "xlu"))
            mm(b("DF1"), b("HI"), b("OX"), False, True)
        tt(b("BE"), ind("LB", 0, 64, "hlu"), b(BA), op.add)
        tt(b("PB"), ind(CMc, 0, 528, "jlu"), b("BE"), op.max)

        def pieces():
            ts(w("p5"), w("np"), 1.0, op.is_lt, 528.0, op.mult)
            ts(w("pz"), w("np"), 1.0, op.is_lt)
            tt(w("cl"), w("p5"), b("KW"), op.add)
            tt(w("lp"), w("h528"), w("pz"), op.mult)
            cp(b("clu"), w("cl"))
            tt(w("ll"), w("lp"), b("KW"), op.max)
            cp(b("llu"), w("ll"))
            cf_old = b("CON") if t == 0 else b("CF%d" % ((t + 1) % 2))
            tt(b("CFI") if last else b("CF%d" % (t % 2)), ind(CMc, 0, 1040, "clu"), cf_old, op.max)

        if last: pieces()
        tt(x("d"), w("h1k"), b("PX", 0, 32), op.subtract)
        ts(x("dd"), x("d"), 8191, op.bitwise_and)
        cp(b("ylu"), x("dd"))
        if not last: send(b("ZO%d" % t), "Z%d" % (t + 1), 0, K, nxt)
        if not last:
            ac(b("NF"), b("DF1"), act.Identity, bias=WHOLE)
            ac(b("NB"), b("NF"), act.Identity, bias=-WHOLE)
        for half, (l0, l1) in enumerate(HALVES):
            yi = ind("Y", 0, 16 * K, "ylu", l0 // 16, l1 // 16)
            tt(b("TY", l0, l1), (yi[0], yall + yi[1][1:]), b("PB", l0, l1), op.max)
            ts(b("SN", l0, l1), b("TY", l0, l1), 8191, op.bitwise_and)
            if not last:
                cp(b("UO%d" % t, l0, l1), b("SN", l0, l1))
                send(b("UO%d" % t, l0, l1), "SU%d" % (t + 1), l0, l1, nxt, "ab"[half])
                if half == 0:
                    si = ind("X", 0, NREC, "xlu")
                    cp((si[0], si[1][:1], si[1][1:]), b("NB"))
        if not last:
            ts(b("EO%d" % t), b("SN"), b("IC"), op.add)
            send(b("EO%d" % t), "SE%d" % (t + 1), 0, K, nxt)
            pieces()
            later.append(lambda a=LWn, c=LWc: ac(b(a, 0, K), ind(c, 0, 560, "llu")))
            later.append(lambda a=CMn, c=CMc: ac(b(a, 0, K), ind(c, 0, 1040, "clu")))
            ts(w("un"), w("h"), 16.0, op.is_ge)
            run("V", lambda: g.vector.tensor_reduce(T.RED[:, :], w("un")[0], AxisListType.X, op.add), b("RED"), [w("un")])
            mm(b("VV", 0, 1), b("ONE"), b("RED"), True, True)
        else:
            cp(b("FO"), b("SN"))
            dma("S", (T.ys[:, :], []), b("FO"), "oS")
            dma("S", (T.yz[:, :], []), b("ZO%d" % t), "oZ")
            ts(b("FI"), b("CFI"), 8191, op.bitwise_and)
            cp(b("FC"), b("FI"))
            dma("S", (T.yc[:, :], []), b("FC"), "oC")
            ac(b(LWn, 0, K), ind(LWc, 0, 560, "llu"))
            ac(b("FN"), b(LWn, 0, K), scale=1.0 / 32.0)
            dma("S", (T.yn[:, :], []), (T.FN[0:128:16, :], [("FN", 0, K)]), "oN")

    for s in SEMAPHORES:
        if total[s]: g.wait_ge(T.sem[s], total[s])
